import numpy as np
import ml_dtypes


def mxq(x, axis, fmt="e4m3"):
    dtype, down = {"e4m3": (ml_dtypes.float8_e4m3fn, 7), "e5m2": (ml_dtypes.float8_e5m2, 14)}[fmt]
    v = np.moveaxis(np.asarray(x, np.float32).astype(ml_dtypes.bfloat16).astype(np.float64), axis, -1)
    blocks = v.reshape(v.shape[:-1] + (-1, 32))
    amax = np.abs(blocks).max(-1, keepdims=True)
    byte = np.maximum(np.where(amax > 0, np.frexp(amax)[1] - 1 + 127, 0) - down, 1)
    scale = np.exp2(byte - 127.0)
    codes = (blocks / scale).astype(np.float32).astype(dtype).astype(np.float64)
    return np.moveaxis((codes * scale).reshape(v.shape), -1, axis)


WIDE = False


def mx_kscale(k):
    if not WIDE:
        return np.ones(k)
    levels = np.array([10, -10, 5, -5, 0])
    if k % 512:
        return np.exp2(np.random.permutation(np.resize(levels, k // 32))).repeat(32)
    a = np.empty((k // 512, 16))
    for p in range(k // 512):
        a[p, :8] = np.random.permutation(np.resize(levels, 8))
        for g in range(8):
            far = levels[np.abs(levels - a[p, g]) >= 10]
            a[p, g + 8] = far[np.random.randint(len(far))]
    return np.exp2(a.ravel()).repeat(32)


def f64(x):
    return np.asarray(x).astype(np.float64)


def striped(idx):
    return np.tile(idx.reshape(-1, 16).T, (8, 1)).astype(np.uint16)


def unstriped(offs):
    return offs[:16].T.reshape(-1).astype(np.int64)


E2M1 = np.array([0.0, 0.5, 1.0, 1.5, 2.0, 3.0, 4.0, 6.0, -0.0, -0.5, -1.0, -1.5, -2.0, -3.0, -4.0, -6.0])


def pack_weight(w, fmt):
    k, n = w.shape
    w = f64(np.asarray(w, np.float32).astype(ml_dtypes.bfloat16)).reshape(k // 32, 32, n)
    amax = np.abs(w).max(1)
    if fmt == "e4m3":
        byte = np.frexp(amax)[1] - 1 + 127 - 7
    else:
        mant, ex = np.frexp(amax / 6.0)
        byte = np.where(mant > 0.5, ex, ex - 1) + 127
    byte = np.clip(np.where(amax > 0, byte, 1), 1, 254)
    scaled = (w * np.exp2(127.0 - byte)[:, None, :]).reshape(k, n).astype(np.float32)
    by_word = np.ascontiguousarray(scaled.reshape(k // 512, 128, 4, n).transpose(0, 1, 3, 2))
    if fmt == "e4m3":
        words = by_word.astype(ml_dtypes.float8_e4m3fn).view(np.uint8)
    else:
        c = by_word.astype(ml_dtypes.float4_e2m1fn).view(np.uint8) & 0xF
        words = (c[..., 0::2] | (c[..., 1::2] << 4)).reshape(k // 512, 128, 2 * n)
    return np.ascontiguousarray(words), np.ascontiguousarray(byte.astype(np.uint8).reshape(k // 512, 16, n))


def unpack_weight(words, scales, fmt):
    g, _, n = scales.shape
    words = np.ascontiguousarray(words).reshape(g, 128, n, -1)
    if fmt == "e4m3":
        vals = words.view(ml_dtypes.float8_e4m3fn).astype(np.float64)
    else:
        nib = np.empty((g, 128, n, 4), np.uint8)
        nib[..., 0::2] = words & 0xF
        nib[..., 1::2] = words >> 4
        vals = E2M1[nib]
    vals = vals * np.repeat(np.exp2(scales.astype(np.float64) - 127.0), 8, axis=1)[..., None]
    return vals.transpose(0, 1, 3, 2).reshape(g * 512, n)


def gelu(v):
    return 0.5 * v * (1.0 + np.tanh(np.sqrt(2.0 / np.pi) * (v + 0.044715 * v**3)))


def bf(x):
    return np.asarray(x, np.float32).astype(ml_dtypes.bfloat16)

def planes(Y):
    n, m = Y.shape
    b = f64(bf(Y)).reshape(n // 32, 32, m)
    amax = np.abs(b).max(1)
    byte = np.clip(np.where(amax > 0, np.frexp(amax)[1] - 1 + 127 - 7, 1), 1, 254)
    codes = (b * np.exp2(127.0 - byte)[:, None, :]).reshape(n, m).astype(np.float32).astype(ml_dtypes.float8_e4m3fn).view(np.uint8)
    words = codes.reshape(n // 512, 128, 4, m).transpose(0, 1, 3, 2)
    return np.ascontiguousarray(words), np.ascontiguousarray(byte.astype(np.uint8).reshape(n // 512, 16, m))


K, T, S, H, N = 1024, 2048, 1024, 512, 1536

def setup_inputs():
    n = np.random.standard_normal
    s = mx_kscale(K)[:, None]
    u = mx_kscale(H)[:, None]
    tab_words, tab_scales = pack_weight(n((K, T)) * s, "e4m3")
    wc = n((K, H)) / np.sqrt(K) / s * u.T
    wu_words, wu_scales = pack_weight(n((K, H)) / np.sqrt(K) / s * u.T, "e2m1")
    gT = n((H, T)) * u
    wd = n((H, N)) / np.sqrt(H) / u * np.exp(0.8 * n(N))
    return {"tab_words": tab_words, "tab_scales": tab_scales,
            "offs": striped(np.random.permutation(T)[:S]),
            "wc": wc.astype(np.float32),
            "wu_words": wu_words, "wu_scales": wu_scales,
            "gT": gT.astype(np.float32), "wd": wd.astype(np.float32)}

def reference(tab_words, tab_scales, offs, wc, wu_words, wu_scales, gT, wd):
    v = unpack_weight(tab_words, tab_scales, "e4m3")[:, unstriped(offs)]
    g = f64(gT)[:, unstriped(offs)]
    wu = unpack_weight(wu_words, wu_scales, "e2m1")
    A = mxq(f64(wc), 0, "e4m3").T @ v
    B = wu.T @ v
    z = g - 0.1 * (B + 3.0 * (A - B))
    y = mxq(f64(wd), 0, "e4m3").T @ mxq(z, 0, "e4m3")
    words, scales = planes(y)
    return y, words, scales

@@ -1,0 +1,274 @@
+from contextlib import ExitStack
+
+import concourse.mybir as mybir
+from concourse.masks import make_identity
+
+K, T, S, H, N = 1024, 2048, 1024, 512, 1536
+FLOPS = 2 * (2 * K * H * S) + 2 * H * N * S
+
+F32 = mybir.dt.float32
+BF16 = mybir.dt.bfloat16
+I32 = mybir.dt.int32
+U32 = mybir.dt.uint32
+U16 = mybir.dt.uint16
+U8 = mybir.dt.uint8
+FP8X4 = mybir.dt.float8_e4m3fn_x4
+FP4X4 = mybir.dt.float4_e2m1fn_x4
+COPY = mybir.ActivationFunctionType.Copy
+ADD = mybir.AluOpType.add
+
+P = 128
+PACK = 4
+KP = P * PACK
+BANK = 512
+HALF = 512
+QUADS = 4
+
+
+def tile_list_guided_latent_decode_kernel(
+    tc, tab_words, tab_scales, offs, wc, wu_words, wu_scales, gT, wd, out_0, out_1, out_2
+):
+    nc = tc.nc
+    passes = K // KP
+    groups = N // KP
+    halves = S // HALF
+    blocks = S // P
+    per_half = HALF // P
+
+    with ExitStack() as ctx:
+        keep = ctx.enter_context(tc.tile_pool(name="keep", bufs=1))
+        ring = ctx.enter_context(tc.tile_pool(name="ring", bufs=2))
+        psum = ctx.enter_context(tc.psum_pool(name="psum", bufs=4))
+
+        offsets = keep.tile([P, S // 16], U16, name="offsets")
+        nc.sync.dma_start(offsets[:], offs)
+
+        tab_s = keep.tile([P, passes * T // 4], I32, name="tab_s", align_bytes=64)
+        nc.gpsimd.memset(tab_s[:, : T // 4], 0)
+        nc.vector.memset(tab_s[:, T // 4 :], 0)
+        wu_s = keep.tile([P, passes * H // 4], I32, name="wu_s", align_bytes=64)
+        nc.vector.memset(wu_s[:], 0)
+        ident = keep.tile([P, P], F32, name="ident")
+        make_identity(nc, ident[:])
+
+        def load_table(a):
+            t = keep.tile([P, T], I32, name="tab_w%d" % a, align_bytes=64)
+            nc.sync.dma_start(t[:], tab_words[a].rearrange("p t i -> p (t i)").bitcast(I32))
+            return t
+
+        def load_wc(a):
+            t = ring.tile([P, PACK, H], F32, name="wc_raw%d" % a, tag="big", bufs=4)
+            nc.sync.dma_start(t[:], wc[a * KP : (a + 1) * KP, :].rearrange("(p j) c -> p j c", j=PACK))
+            return t
+
+        def load_g(t):
+            x = keep.tile([P, T], F32, name="g_tab%d" % t)
+            nc.sync.dma_start(x[:], gT.rearrange("(p t) c -> p t c", t=PACK)[:, t, :])
+            return x
+
+        def load_wd(g):
+            x = keep.tile([P, PACK, KP], F32, name="wd_raw%d" % g)
+            nc.sync.dma_start(x[:], wd[:, g * KP : (g + 1) * KP].rearrange("(p j) c -> p j c", j=PACK))
+            return x
+
+        ts32 = tab_scales.bitcast(I32)
+        for q in range(QUADS):
+            nc.sync.dma_start(
+                tab_s[32 * q : 32 * q + 4, :].rearrange("r (a n) -> r a n", a=passes),
+                ts32[:, 4 * q : 4 * q + 4, :].rearrange("a r n -> r a n"),
+            )
+        tab_w = [load_table(0)]
+        wc_raw = [load_wc(0)]
+        tab_w.append(load_table(1))
+        us32 = wu_scales.bitcast(I32)
+        for q in range(QUADS):
+            nc.sync.dma_start(
+                wu_s[32 * q : 32 * q + 4, :].rearrange("r (a n) -> r a n", a=passes),
+                us32[:, 4 * q : 4 * q + 4, :].rearrange("a r n -> r a n"),
+            )
+        wc_raw.append(load_wc(1))
+        wu_w = keep.tile([P, passes, 2 * H // 4], I32, name="wu_w", align_bytes=64)
+        nc.sync.dma_start(wu_w[:], wu_words.bitcast(I32).rearrange("a p n -> p a n"))
+
+        v_w = [keep.tile([P, S], U32, name="v_w%d" % a, align_bytes=64) for a in range(passes)]
+        hcols = HALF // 16
+
+        def gather_words(a, h):
+            nc.vector.tensor_copy(
+                v_w[a][:, h * HALF : (h + 1) * HALF],
+                tab_w[a][:].bitcast(U32).indirect(offsets[:, h * hcols : (h + 1) * hcols]),
+            )
+
+        v_s = [keep.tile([P, S], U8, name="v_s%d" % a, align_bytes=64) for a in range(passes)]
+        for a in range(passes):
+            nc.vector.tensor_copy(v_s[a][:], tab_s[:].bitcast(U8)[:, a * T : (a + 1) * T].indirect(offsets[:]))
+            for h in range(halves):
+                gather_words(a, h)
+
+        wc_q = []
+        for a in range(passes):
+            w16 = ring.tile([P, H * PACK], BF16, name="w16", tag="w16", align_bytes=64)
+            nc.scalar.copy(
+                w16[:].rearrange("p (c i j) -> p c j i", i=4, j=PACK),
+                wc_raw[a][:].rearrange("p j (c i) -> p c j i", i=4),
+            )
+            codes = keep.tile([P, H], U32, name="wc_c%d" % a, align_bytes=64)
+            scales = keep.tile([P, H], U8, name="wc_s%d" % a, align_bytes=64)
+            nc.vector.quantize_mx(out=codes[:].bitcast(FP8X4), scales=scales[:], in_=w16[:])
+            wc_q.append((codes, scales))
+
+        g_tab = [load_g(t) for t in range(PACK)]
+        wd_raw = [load_wd(g) for g in range(groups)]
+
+        g_pick = [keep.tile([P, PACK, HALF], F32, name="g_pick%d" % h) for h in range(halves)]
+
+        def gather_g(t, h):
+            cols = HALF // 16
+            nc.vector.tensor_copy(g_pick[h][:, t, :], g_tab[t][:].indirect(offsets[:, h * cols : (h + 1) * cols]))
+
+        wu_s_bytes = wu_s[:].bitcast(U8)
+        scaled = {}
+
+        def predict(b):
+            cols = slice(b * P, (b + 1) * P)
+            bank_b = psum.tile([P, BANK], F32, name="bank_b", tag="mm")
+            for a in range(passes):
+                nc.tensor.matmul_mx(
+                    out=bank_b[:],
+                    lhsT=v_w[a][:, cols].bitcast(FP8X4),
+                    lhsT_scale=v_s[a][:, cols],
+                    rhs=wu_w[:, a, :].bitcast(FP4X4),
+                    rhs_scale=wu_s_bytes[:, a * H : (a + 1) * H],
+                    start=(a == 0),
+                    stop=(a == passes - 1),
+                )
+            bank_a = psum.tile([P, BANK], F32, name="bank_a", tag="mm")
+            for a in range(passes):
+                nc.tensor.matmul_mx(
+                    out=bank_a[:],
+                    lhsT=v_w[a][:, cols].bitcast(FP8X4),
+                    lhsT_scale=v_s[a][:, cols],
+                    rhs=wc_q[a][0][:].bitcast(FP8X4),
+                    rhs_scale=wc_q[a][1][:],
+                    start=(a == 0),
+                    stop=(a == passes - 1),
+                )
+            pair = []
+            for bank, factor, name in ((bank_b, 0.2, "sb"), (bank_a, -0.3, "sa")):
+                x = keep.tile([P, PACK, P], F32, name="%s%d" % (name, b))
+                nc.scalar.activation(x[:], bank[:].rearrange("p (m t) -> p t m", t=PACK), COPY, scale=factor)
+                pair.append(x)
+            scaled[b] = pair
+
+        turned = {}
+
+        def turn(b):
+            u = psum.tile([P, PACK, P], F32, name="u", tag="u")
+            for t in range(PACK):
+                for i, x in enumerate(scaled[b]):
+                    nc.tensor.matmul(u[:, t, :], x[:, t, :], ident[:], start=(i == 0), stop=(i == 1), is_transpose=True)
+            turned[b] = u
+
+        z16 = [keep.tile([P, HALF * PACK], BF16, name="z16_%d" % h, align_bytes=64) for h in range(halves)]
+
+        def add_latents(b):
+            h, r = divmod(b, per_half)
+            nc.vector.tensor_tensor(
+                z16[h][:, r * KP : (r + 1) * KP].rearrange("p (c i t) -> p c t i", i=4, t=PACK),
+                turned[b][:].rearrange("p t (c i) -> p c t i", i=4),
+                g_pick[h][:, :, r * P : (r + 1) * P].rearrange("p t (c i) -> p c t i", i=4),
+                ADD,
+            )
+
+        z_q = {}
+
+        def quantize_z(h):
+            codes = keep.tile([P, HALF], U32, name="z_c%d" % h, align_bytes=64)
+            scales = keep.tile([P, HALF], U8, name="z_s%d" % h, align_bytes=64)
+            nc.vector.quantize_mx(out=codes[:].bitcast(FP8X4), scales=scales[:], in_=z16[h][:])
+            z_q[h] = (codes, scales)
+
+        wd_q = {}
+
+        def quantize_wd(g):
+            w16 = ring.tile([P, KP * PACK], BF16, name="w16", tag="w16", align_bytes=64)
+            nc.scalar.copy(
+                w16[:].rearrange("p (t m j) -> p m j t", t=PACK, j=PACK),
+                wd_raw[g][:].rearrange("p j (m t) -> p m j t", t=PACK),
+            )
+            codes = keep.tile([P, KP], U32, name="wd_c%d" % g, align_bytes=64)
+            scales = keep.tile([P, KP], U8, name="wd_s%d" % g, align_bytes=64)
+            nc.vector.quantize_mx(out=codes[:].bitcast(FP8X4), scales=scales[:], in_=w16[:])
+            wd_q[g] = (codes, scales)
+
+        y_s = [keep.tile([P, groups * HALF], U8, name="y_s%d" % h, align_bytes=64) for h in range(halves)]
+        words32 = out_1.rearrange("g p m t -> g p (m t)").bitcast(I32)
+        scales32 = out_2.bitcast(I32)
+
+        def project(h, g):
+            cols = slice(h * HALF, (h + 1) * HALF)
+            y = ring.tile([P, PACK, HALF], F32, name="y", tag="big", bufs=4)
+            rows = out_0[g * KP : (g + 1) * KP, cols].rearrange("(p t) s -> p t s", t=PACK)
+            for t in range(PACK):
+                bank = psum.tile([P, BANK], F32, name="bank_y", tag="mm")
+                wcols = slice(t * P, (t + 1) * P)
+                nc.tensor.matmul_mx(
+                    out=bank[:],
+                    lhsT=wd_q[g][0][:, wcols].bitcast(FP8X4),
+                    lhsT_scale=wd_q[g][1][:, wcols],
+                    rhs=z_q[h][0][:].bitcast(FP8X4),
+                    rhs_scale=z_q[h][1][:],
+                    start=True,
+                    stop=True,
+                )
+                nc.scalar.copy(y[:, t, :], bank[:])
+                if t % 2 == 1:
+                    nc.sync.dma_start(rows[:, t - 1 : t + 1, :], y[:, t - 1 : t + 1, :])
+            y16 = ring.tile([P, HALF * PACK], BF16, name="y16", align_bytes=64)
+            nc.vector.tensor_copy(
+                y16[:].rearrange("p (c i t) -> p c t i", i=4, t=PACK),
+                y[:].rearrange("p t (c i) -> p c t i", i=4),
+            )
+            codes = ring.tile([P, HALF], U32, name="y_c", align_bytes=64, bufs=3)
+            nc.vector.quantize_mx(
+                out=codes[:].bitcast(FP8X4), scales=y_s[h][:, g * HALF : (g + 1) * HALF], in_=y16[:]
+            )
+            nc.sync.dma_start(words32[g][:, cols], codes[:].bitcast(I32))
+
+        def store_scales(h):
+            w = HALF // 4
+            for q in range(QUADS):
+                nc.scalar.dma_start(
+                    scales32[:, 4 * q : 4 * q + 4, h * w : (h + 1) * w].rearrange("g r n -> r g n"),
+                    y_s[h][32 * q : 32 * q + 4, :].bitcast(I32).rearrange("r (g n) -> r g n", g=groups),
+                )
+
+        for b in range(per_half):
+            predict(b)
+        for b in range(per_half):
+            turn(b)
+        for t in range(PACK - 1):
+            gather_g(t, 0)
+            gather_g(t, 1)
+        gather_g(PACK - 1, 0)
+        for b in range(per_half):
+            add_latents(b)
+        quantize_z(0)
+        quantize_wd(0)
+        for b in range(per_half, blocks):
+            predict(b)
+        gather_g(PACK - 1, 1)
+        project(0, 0)
+        for b in range(per_half, blocks):
+            turn(b)
+            add_latents(b)
+        quantize_z(1)
+        quantize_wd(1)
+        project(1, 0)
+        quantize_wd(2)
+        project(0, 1)
+        project(0, 2)
+        project(1, 1)
+        store_scales(0)
+        project(1, 2)
+        store_scales(1)

@@ -72,23 +72,31 @@ def tile_list_guided_latent_decode_kernel(
             return x
 
         ts32 = tab_scales.bitcast(I32)
-        for q in range(QUADS):
-            nc.sync.dma_start(
-                tab_s[32 * q : 32 * q + 4, :].rearrange("r (a n) -> r a n", a=passes),
-                ts32[:, 4 * q : 4 * q + 4, :].rearrange("a r n -> r a n"),
-            )
-        tab_w = [load_table(0)]
-        wc_raw = [load_wc(0)]
-        tab_w.append(load_table(1))
         us32 = wu_scales.bitcast(I32)
-        for q in range(QUADS):
-            nc.sync.dma_start(
-                wu_s[32 * q : 32 * q + 4, :].rearrange("r (a n) -> r a n", a=passes),
-                us32[:, 4 * q : 4 * q + 4, :].rearrange("a r n -> r a n"),
-            )
-        wc_raw.append(load_wc(1))
         wu_w = keep.tile([P, passes, 2 * H // 4], I32, name="wu_w", align_bytes=64)
+
+        def load_planes(tile, rows):
+            for q in range(QUADS):
+                nc.sync.dma_start(
+                    tile[32 * q : 32 * q + 4, :].rearrange("r (a n) -> r a n", a=passes),
+                    rows[:, 4 * q : 4 * q + 4, :].rearrange("a r n -> r a n"),
+                )
+
+        tab_w, wc_raw, g_tab, wd_raw = {}, {}, {}, {}
+        load_planes(tab_s, ts32)
+        tab_w[0] = load_table(0)
+        wc_raw[0] = load_wc(0)
+        tab_w[1] = load_table(1)
+        load_planes(wu_s, us32)
+        wc_raw[1] = load_wc(1)
         nc.sync.dma_start(wu_w[:], wu_words.bitcast(I32).rearrange("a p n -> p a n"))
+        g_tab[0] = load_g(0)
+        g_tab[1] = load_g(1)
+        g_tab[2] = load_g(2)
+        g_tab[3] = load_g(3)
+        wd_raw[0] = load_wd(0)
+        wd_raw[1] = load_wd(1)
+        wd_raw[2] = load_wd(2)
 
         v_w = [keep.tile([P, S], U32, name="v_w%d" % a, align_bytes=64) for a in range(passes)]
         hcols = HALF // 16
@@ -109,16 +117,14 @@ def tile_list_guided_latent_decode_kernel(
         for a in range(passes):
             w16 = ring.tile([P, H * PACK], BF16, name="w16", tag="w16", align_bytes=64)
             nc.scalar.copy(
-                w16[:].rearrange("p (c i j) -> p c j i", i=4, j=PACK),
-                wc_raw[a][:].rearrange("p j (c i) -> p c j i", i=4),
+                w16[:].rearrange("p (c i j) -> p c j i", i=2, j=PACK),
+                wc_raw[a][:].rearrange("p j (c i) -> p c j i", i=2),
             )
             codes = keep.tile([P, H], U32, name="wc_c%d" % a, align_bytes=64)
             scales = keep.tile([P, H], U8, name="wc_s%d" % a, align_bytes=64)
             nc.vector.quantize_mx(out=codes[:].bitcast(FP8X4), scales=scales[:], in_=w16[:])
             wc_q.append((codes, scales))
 
-        g_tab = [load_g(t) for t in range(PACK)]
-        wd_raw = [load_wd(g) for g in range(groups)]
 
         g_pick = [keep.tile([P, PACK, HALF], F32, name="g_pick%d" % h) for h in range(halves)]
 
@@ -131,7 +137,7 @@ def tile_list_guided_latent_decode_kernel(
 
         def predict(b):
             cols = slice(b * P, (b + 1) * P)
-            bank_b = psum.tile([P, BANK], F32, name="bank_b", tag="mm")
+            bank_b = psum.tile([P, BANK], F32, name="bank_b", tag="mm", bufs=4)
             for a in range(passes):
                 nc.tensor.matmul_mx(
                     out=bank_b[:],
@@ -142,7 +148,7 @@ def tile_list_guided_latent_decode_kernel(
                     start=(a == 0),
                     stop=(a == passes - 1),
                 )
-            bank_a = psum.tile([P, BANK], F32, name="bank_a", tag="mm")
+            bank_a = psum.tile([P, BANK], F32, name="bank_a", tag="mm", bufs=4)
             for a in range(passes):
                 nc.tensor.matmul_mx(
                     out=bank_a[:],
@@ -156,14 +162,19 @@ def tile_list_guided_latent_decode_kernel(
             pair = []
             for bank, factor, name in ((bank_b, 0.2, "sb"), (bank_a, -0.3, "sa")):
                 x = keep.tile([P, PACK, P], F32, name="%s%d" % (name, b))
-                nc.scalar.activation(x[:], bank[:].rearrange("p (m t) -> p t m", t=PACK), COPY, scale=factor)
+                nc.scalar.activation(
+                    x[:].rearrange("p (u e) m -> p u m e", e=2),
+                    bank[:].rearrange("p (m u e) -> p u m e", u=2, e=2),
+                    COPY,
+                    scale=factor,
+                )
                 pair.append(x)
             scaled[b] = pair
 
         turned = {}
 
         def turn(b):
-            u = psum.tile([P, PACK, P], F32, name="u", tag="u")
+            u = psum.tile([P, PACK, P], F32, name="u", tag="u", bufs=4)
             for t in range(PACK):
                 for i, x in enumerate(scaled[b]):
                     nc.tensor.matmul(u[:, t, :], x[:, t, :], ident[:], start=(i == 0), stop=(i == 1), is_transpose=True)
@@ -174,27 +185,29 @@ def tile_list_guided_latent_decode_kernel(
         def add_latents(b):
             h, r = divmod(b, per_half)
             nc.vector.tensor_tensor(
-                z16[h][:, r * KP : (r + 1) * KP].rearrange("p (c i t) -> p c t i", i=4, t=PACK),
-                turned[b][:].rearrange("p t (c i) -> p c t i", i=4),
-                g_pick[h][:, :, r * P : (r + 1) * P].rearrange("p t (c i) -> p c t i", i=4),
+                z16[h][:, r * KP : (r + 1) * KP].rearrange("p (c i t) -> p c t i", i=2, t=PACK),
+                turned[b][:].rearrange("p t (c i) -> p c t i", i=2),
+                g_pick[h][:, :, r * P : (r + 1) * P].rearrange("p t (c i) -> p c t i", i=2),
                 ADD,
             )
 
-        z_q = {}
+        z_c = [keep.tile([P, HALF], U32, name="z_c%d" % h, align_bytes=64) for h in range(halves)]
+        z_s = [keep.tile([P, HALF], U8, name="z_s%d" % h, align_bytes=64) for h in range(halves)]
 
-        def quantize_z(h):
-            codes = keep.tile([P, HALF], U32, name="z_c%d" % h, align_bytes=64)
-            scales = keep.tile([P, HALF], U8, name="z_s%d" % h, align_bytes=64)
-            nc.vector.quantize_mx(out=codes[:].bitcast(FP8X4), scales=scales[:], in_=z16[h][:])
-            z_q[h] = (codes, scales)
+        def quantize_z(h, c0, width):
+            nc.vector.quantize_mx(
+                out=z_c[h][:, c0 : c0 + width].bitcast(FP8X4),
+                scales=z_s[h][:, c0 : c0 + width],
+                in_=z16[h][:, PACK * c0 : PACK * (c0 + width)],
+            )
 
         wd_q = {}
 
-        def quantize_wd(g):
+        def quantize_wd(g, copy):
             w16 = ring.tile([P, KP * PACK], BF16, name="w16", tag="w16", align_bytes=64)
-            nc.scalar.copy(
-                w16[:].rearrange("p (t m j) -> p m j t", t=PACK, j=PACK),
-                wd_raw[g][:].rearrange("p j (m t) -> p m j t", t=PACK),
+            copy(
+                w16[:].rearrange("p (u e m j) -> p u m j e", u=2, e=2, j=PACK),
+                wd_raw[g][:].rearrange("p j (m u e) -> p u m j e", u=2, e=2),
             )
             codes = keep.tile([P, KP], U32, name="wd_c%d" % g, align_bytes=64)
             scales = keep.tile([P, KP], U8, name="wd_s%d" % g, align_bytes=64)
@@ -205,33 +218,37 @@ def tile_list_guided_latent_decode_kernel(
         words32 = out_1.rearrange("g p m t -> g p (m t)").bitcast(I32)
         scales32 = out_2.bitcast(I32)
 
-        def project(h, g):
-            cols = slice(h * HALF, (h + 1) * HALF)
-            y = ring.tile([P, PACK, HALF], F32, name="y", tag="big", bufs=4)
+        def project(h, g, c0, width):
+            local = slice(c0, c0 + width)
+            cols = slice(h * HALF + c0, h * HALF + c0 + width)
+            y = ring.tile([P, PACK, width], F32, name="y", tag="big", bufs=4)
             rows = out_0[g * KP : (g + 1) * KP, cols].rearrange("(p t) s -> p t s", t=PACK)
-            for t in range(PACK):
-                bank = psum.tile([P, BANK], F32, name="bank_y", tag="mm")
-                wcols = slice(t * P, (t + 1) * P)
-                nc.tensor.matmul_mx(
-                    out=bank[:],
-                    lhsT=wd_q[g][0][:, wcols].bitcast(FP8X4),
-                    lhsT_scale=wd_q[g][1][:, wcols],
-                    rhs=z_q[h][0][:].bitcast(FP8X4),
-                    rhs_scale=z_q[h][1][:],
-                    start=True,
-                    stop=True,
-                )
-                nc.scalar.copy(y[:, t, :], bank[:])
-                if t % 2 == 1:
-                    nc.sync.dma_start(rows[:, t - 1 : t + 1, :], y[:, t - 1 : t + 1, :])
-            y16 = ring.tile([P, HALF * PACK], BF16, name="y16", align_bytes=64)
+            per_bank = BANK // width
+            for t0 in range(0, PACK, per_bank):
+                bank = psum.tile([P, per_bank, width], F32, name="bank_y", tag="mm", bufs=4)
+                for j in range(per_bank):
+                    wcols = slice((t0 + j) * P, (t0 + j + 1) * P)
+                    nc.tensor.matmul_mx(
+                        out=bank[:, j, :],
+                        lhsT=wd_q[g][0][:, wcols].bitcast(FP8X4),
+                        lhsT_scale=wd_q[g][1][:, wcols],
+                        rhs=z_c[h][:, local].bitcast(FP8X4),
+                        rhs_scale=z_s[h][:, local],
+                        start=True,
+                        stop=True,
+                    )
+                nc.scalar.copy(y[:, t0 : t0 + per_bank, :], bank[:])
+                t1 = t0 + per_bank
+                if t1 % 2 == 0:
+                    nc.sync.dma_start(rows[:, t1 - 2 : t1, :], y[:, t1 - 2 : t1, :])
+            y16 = ring.tile([P, width * PACK], BF16, name="y16", align_bytes=64)
             nc.vector.tensor_copy(
-                y16[:].rearrange("p (c i t) -> p c t i", i=4, t=PACK),
-                y[:].rearrange("p t (c i) -> p c t i", i=4),
+                y16[:].rearrange("p (c i t) -> p c t i", i=2, t=PACK),
+                y[:].rearrange("p t (c i) -> p c t i", i=2),
             )
-            codes = ring.tile([P, HALF], U32, name="y_c", align_bytes=64, bufs=3)
+            codes = ring.tile([P, width], U32, name="y_c", align_bytes=64, bufs=3)
             nc.vector.quantize_mx(
-                out=codes[:].bitcast(FP8X4), scales=y_s[h][:, g * HALF : (g + 1) * HALF], in_=y16[:]
+                out=codes[:].bitcast(FP8X4), scales=y_s[h][:, g * HALF + c0 : g * HALF + c0 + width], in_=y16[:]
             )
             nc.sync.dma_start(words32[g][:, cols], codes[:].bitcast(I32))
 
@@ -243,6 +260,8 @@ def tile_list_guided_latent_decode_kernel(
                     y_s[h][32 * q : 32 * q + 4, :].bitcast(I32).rearrange("r (g n) -> r g n", g=groups),
                 )
 
+        quarter = HALF // 2
+        on_s, on_v = nc.scalar.copy, nc.vector.tensor_copy
         for b in range(per_half):
             predict(b)
         for b in range(per_half):
@@ -253,22 +272,22 @@ def tile_list_guided_latent_decode_kernel(
         gather_g(PACK - 1, 0)
         for b in range(per_half):
             add_latents(b)
-        quantize_z(0)
-        quantize_wd(0)
+        quantize_z(0, 0, HALF)
+        quantize_wd(0, on_s)
         for b in range(per_half, blocks):
             predict(b)
         gather_g(PACK - 1, 1)
-        project(0, 0)
+        project(0, 0, 0, HALF)
         for b in range(per_half, blocks):
             turn(b)
             add_latents(b)
-        quantize_z(1)
-        quantize_wd(1)
-        project(1, 0)
-        quantize_wd(2)
-        project(0, 1)
-        project(0, 2)
-        project(1, 1)
+        quantize_z(1, 0, HALF)
+        quantize_wd(1, on_s)
+        project(1, 0, 0, HALF)
+        quantize_wd(2, on_s)
+        project(0, 1, 0, HALF)
+        project(0, 2, 0, HALF)
+        project(1, 1, 0, HALF)
         store_scales(0)
-        project(1, 2)
+        project(1, 2, 0, HALF)
         store_scales(1)

@@ -38,7 +38,7 @@ def tile_list_guided_latent_decode_kernel(
     with ExitStack() as ctx:
         keep = ctx.enter_context(tc.tile_pool(name="keep", bufs=1))
         ring = ctx.enter_context(tc.tile_pool(name="ring", bufs=2))
-        psum = ctx.enter_context(tc.psum_pool(name="psum", bufs=4))
+        psum = ctx.enter_context(tc.psum_pool(name="psum", bufs=1))
 
         offsets = keep.tile([P, S // 16], U16, name="offsets")
         nc.sync.dma_start(offsets[:], offs)
@@ -57,7 +57,7 @@ def tile_list_guided_latent_decode_kernel(
             return t
 
         def load_wc(a):
-            t = ring.tile([P, PACK, H], F32, name="wc_raw%d" % a, tag="big", bufs=4)
+            t = ring.tile([P, PACK, H], F32, name="wc_raw%d" % a, tag="big", bufs=7)
             nc.sync.dma_start(t[:], wc[a * KP : (a + 1) * KP, :].rearrange("(p j) c -> p j c", j=PACK))
             return t
 
@@ -67,7 +67,7 @@ def tile_list_guided_latent_decode_kernel(
             return x
 
         def load_wd(g):
-            x = keep.tile([P, PACK, KP], F32, name="wd_raw%d" % g)
+            x = ring.tile([P, PACK, KP], F32, name="wd_raw%d" % g, tag="big", bufs=7)
             nc.sync.dma_start(x[:], wd[:, g * KP : (g + 1) * KP].rearrange("(p j) c -> p j c", j=PACK))
             return x
 
@@ -76,19 +76,17 @@ def tile_list_guided_latent_decode_kernel(
         wu_w = keep.tile([P, passes, 2 * H // 4], I32, name="wu_w", align_bytes=64)
 
         def load_planes(tile, rows):
-            for q in range(QUADS):
-                nc.sync.dma_start(
-                    tile[32 * q : 32 * q + 4, :].rearrange("r (a n) -> r a n", a=passes),
-                    rows[:, 4 * q : 4 * q + 4, :].rearrange("a r n -> r a n"),
-                )
+            by_row = rows.rearrange("a (q r) n -> r q a n", r=4)
+            for r in range(4):
+                nc.sync.dma_start(tile[r:P:32, :].rearrange("q (a n) -> q a n", a=passes), by_row[r])
 
         tab_w, wc_raw, g_tab, wd_raw = {}, {}, {}, {}
         load_planes(tab_s, ts32)
         tab_w[0] = load_table(0)
         wc_raw[0] = load_wc(0)
         tab_w[1] = load_table(1)
-        load_planes(wu_s, us32)
         wc_raw[1] = load_wc(1)
+        load_planes(wu_s, us32)
         nc.sync.dma_start(wu_w[:], wu_words.bitcast(I32).rearrange("a p n -> p a n"))
         g_tab[0] = load_g(0)
         g_tab[1] = load_g(1)
@@ -128,53 +126,47 @@ def tile_list_guided_latent_decode_kernel(
 
         g_pick = [keep.tile([P, PACK, HALF], F32, name="g_pick%d" % h) for h in range(halves)]
 
-        def gather_g(t, h):
-            cols = HALF // 16
-            nc.vector.tensor_copy(g_pick[h][:, t, :], g_tab[t][:].indirect(offsets[:, h * cols : (h + 1) * cols]))
+        def gather_g(t, h, c0=0, width=HALF):
+            first = (h * HALF + c0) // 16
+            nc.vector.tensor_copy(
+                g_pick[h][:, t, c0 : c0 + width], g_tab[t][:].indirect(offsets[:, first : first + width // 16])
+            )
 
         wu_s_bytes = wu_s[:].bitcast(U8)
         scaled = {}
 
-        def predict(b):
+        banks = [psum.tile([P, BANK], F32, name="bank%d" % i) for i in range(8)]
+
+        def predict(b, which, bank):
             cols = slice(b * P, (b + 1) * P)
-            bank_b = psum.tile([P, BANK], F32, name="bank_b", tag="mm", bufs=4)
-            for a in range(passes):
+            order = range(passes) if which == "b" else range(passes - 1, -1, -1)
+            for i, a in enumerate(order):
+                if which == "b":
+                    rhs, rhs_scale = wu_w[:, a, :].bitcast(FP4X4), wu_s_bytes[:, a * H : (a + 1) * H]
+                else:
+                    rhs, rhs_scale = wc_q[a][0][:].bitcast(FP8X4), wc_q[a][1][:]
                 nc.tensor.matmul_mx(
-                    out=bank_b[:],
+                    out=bank[:],
                     lhsT=v_w[a][:, cols].bitcast(FP8X4),
                     lhsT_scale=v_s[a][:, cols],
-                    rhs=wu_w[:, a, :].bitcast(FP4X4),
-                    rhs_scale=wu_s_bytes[:, a * H : (a + 1) * H],
-                    start=(a == 0),
-                    stop=(a == passes - 1),
+                    rhs=rhs,
+                    rhs_scale=rhs_scale,
+                    start=(i == 0),
+                    stop=(i == passes - 1),
                 )
-            bank_a = psum.tile([P, BANK], F32, name="bank_a", tag="mm", bufs=4)
-            for a in range(passes):
-                nc.tensor.matmul_mx(
-                    out=bank_a[:],
-                    lhsT=v_w[a][:, cols].bitcast(FP8X4),
-                    lhsT_scale=v_s[a][:, cols],
-                    rhs=wc_q[a][0][:].bitcast(FP8X4),
-                    rhs_scale=wc_q[a][1][:],
-                    start=(a == 0),
-                    stop=(a == passes - 1),
-                )
-            pair = []
-            for bank, factor, name in ((bank_b, 0.2, "sb"), (bank_a, -0.3, "sa")):
-                x = keep.tile([P, PACK, P], F32, name="%s%d" % (name, b))
-                nc.scalar.activation(
-                    x[:].rearrange("p (u e) m -> p u m e", e=2),
-                    bank[:].rearrange("p (m u e) -> p u m e", u=2, e=2),
-                    COPY,
-                    scale=factor,
-                )
-                pair.append(x)
-            scaled[b] = pair
+            x = keep.tile([P, PACK, P], F32, name="s%s%d" % (which, b))
+            nc.scalar.activation(
+                x[:].rearrange("p (u e) m -> p u m e", e=2),
+                bank[:].rearrange("p (m u e) -> p u m e", u=2, e=2),
+                COPY,
+                scale=0.2 if which == "b" else -0.3,
+            )
+            scaled.setdefault(b, []).append(x)
 
         turned = {}
 
-        def turn(b):
-            u = psum.tile([P, PACK, P], F32, name="u", tag="u", bufs=4)
+        def turn(b, bank):
+            u = bank[:].rearrange("p (t s) -> p t s", t=PACK)
             for t in range(PACK):
                 for i, x in enumerate(scaled[b]):
                     nc.tensor.matmul(u[:, t, :], x[:, t, :], ident[:], start=(i == 0), stop=(i == 1), is_transpose=True)
@@ -186,7 +178,7 @@ def tile_list_guided_latent_decode_kernel(
             h, r = divmod(b, per_half)
             nc.vector.tensor_tensor(
                 z16[h][:, r * KP : (r + 1) * KP].rearrange("p (c i t) -> p c t i", i=2, t=PACK),
-                turned[b][:].rearrange("p t (c i) -> p c t i", i=2),
+                turned[b].rearrange("p t (c i) -> p c t i", i=2),
                 g_pick[h][:, :, r * P : (r + 1) * P].rearrange("p t (c i) -> p c t i", i=2),
                 ADD,
             )
@@ -203,29 +195,30 @@ def tile_list_guided_latent_decode_kernel(
 
         wd_q = {}
 
-        def quantize_wd(g, copy):
+        def quantize_wd(g, copies):
             w16 = ring.tile([P, KP * PACK], BF16, name="w16", tag="w16", align_bytes=64)
-            copy(
-                w16[:].rearrange("p (u e m j) -> p u m j e", u=2, e=2, j=PACK),
-                wd_raw[g][:].rearrange("p j (m u e) -> p u m j e", u=2, e=2),
-            )
+            for u, copy in enumerate(copies):
+                copy(
+                    w16[:].rearrange("p (u e m j) -> p u m j e", u=2, e=2, j=PACK)[:, u],
+                    wd_raw[g][:].rearrange("p j (m u e) -> p u m j e", u=2, e=2)[:, u],
+                )
             codes = keep.tile([P, KP], U32, name="wd_c%d" % g, align_bytes=64)
             scales = keep.tile([P, KP], U8, name="wd_s%d" % g, align_bytes=64)
             nc.vector.quantize_mx(out=codes[:].bitcast(FP8X4), scales=scales[:], in_=w16[:])
             wd_q[g] = (codes, scales)
 
-        y_s = [keep.tile([P, groups * HALF], U8, name="y_s%d" % h, align_bytes=64) for h in range(halves)]
+        y_s = keep.tile([P, groups * S], U8, name="y_s", align_bytes=64)
         words32 = out_1.rearrange("g p m t -> g p (m t)").bitcast(I32)
         scales32 = out_2.bitcast(I32)
 
-        def project(h, g, c0, width):
+        def project(h, g, c0, width, free, step=2):
             local = slice(c0, c0 + width)
             cols = slice(h * HALF + c0, h * HALF + c0 + width)
-            y = ring.tile([P, PACK, width], F32, name="y", tag="big", bufs=4)
+            y = ring.tile([P, PACK, width], F32, name="y", tag="big", bufs=7)
             rows = out_0[g * KP : (g + 1) * KP, cols].rearrange("(p t) s -> p t s", t=PACK)
             per_bank = BANK // width
             for t0 in range(0, PACK, per_bank):
-                bank = psum.tile([P, per_bank, width], F32, name="bank_y", tag="mm", bufs=4)
+                bank = free[t0 // per_bank][:].rearrange("p (j s) -> p j s", j=per_bank)
                 for j in range(per_bank):
                     wcols = slice((t0 + j) * P, (t0 + j + 1) * P)
                     nc.tensor.matmul_mx(
@@ -237,57 +230,62 @@ def tile_list_guided_latent_decode_kernel(
                         start=True,
                         stop=True,
                     )
-                nc.scalar.copy(y[:, t0 : t0 + per_bank, :], bank[:])
+                nc.scalar.copy(y[:, t0 : t0 + per_bank, :], bank)
                 t1 = t0 + per_bank
-                if t1 % 2 == 0:
-                    nc.sync.dma_start(rows[:, t1 - 2 : t1, :], y[:, t1 - 2 : t1, :])
+                if t1 % step == 0:
+                    nc.sync.dma_start(rows[:, t1 - step : t1, :], y[:, t1 - step : t1, :])
+            return y, h, g, c0, width
+
+        def planes(unit, weave=nc.vector.tensor_copy):
+            y, h, g, c0, width = unit
+            cols = slice(h * HALF + c0, h * HALF + c0 + width)
             y16 = ring.tile([P, width * PACK], BF16, name="y16", align_bytes=64)
-            nc.vector.tensor_copy(
+            weave(
                 y16[:].rearrange("p (c i t) -> p c t i", i=2, t=PACK),
                 y[:].rearrange("p t (c i) -> p c t i", i=2),
             )
-            codes = ring.tile([P, width], U32, name="y_c", align_bytes=64, bufs=3)
+            codes = ring.tile([P, width], U32, name="y_c", align_bytes=64, bufs=6)
             nc.vector.quantize_mx(
-                out=codes[:].bitcast(FP8X4), scales=y_s[h][:, g * HALF + c0 : g * HALF + c0 + width], in_=y16[:]
+                out=codes[:].bitcast(FP8X4), scales=y_s[:, g * S + cols.start : g * S + cols.stop], in_=y16[:]
             )
             nc.sync.dma_start(words32[g][:, cols], codes[:].bitcast(I32))
 
-        def store_scales(h):
-            w = HALF // 4
-            for q in range(QUADS):
-                nc.scalar.dma_start(
-                    scales32[:, 4 * q : 4 * q + 4, h * w : (h + 1) * w].rearrange("g r n -> r g n"),
-                    y_s[h][32 * q : 32 * q + 4, :].bitcast(I32).rearrange("r (g n) -> r g n", g=groups),
-                )
+        def store_scales(queue):
+            by_row = scales32.rearrange("g (q r) n -> r q g n", r=4)
+            for r in range(4):
+                queue.dma_start(by_row[r], y_s[r:P:32, :].bitcast(I32).rearrange("q (g n) -> q g n", g=groups))
 
         quarter = HALF // 2
         on_s, on_v = nc.scalar.copy, nc.vector.tensor_copy
-        for b in range(per_half):
-            predict(b)
-        for b in range(per_half):
-            turn(b)
+        low, high = banks[:4], banks[4:]
+        for h in range(halves):
+            for r in range(per_half):
+                predict(h * per_half + r, "b", low[r])
+            for r in range(per_half):
+                predict(h * per_half + r, "a", high[r])
+        for r in range(per_half):
+            turn(r, low[r])
         for t in range(PACK - 1):
             gather_g(t, 0)
             gather_g(t, 1)
         gather_g(PACK - 1, 0)
-        for b in range(per_half):
-            add_latents(b)
+        quantize_wd(0, (on_s, on_s))
+        for r in range(per_half):
+            add_latents(r)
         quantize_z(0, 0, HALF)
-        quantize_wd(0, on_s)
-        for b in range(per_half, blocks):
-            predict(b)
+        units = [project(0, 0, 0, HALF, high, 1)]
         gather_g(PACK - 1, 1)
-        project(0, 0, 0, HALF)
-        for b in range(per_half, blocks):
-            turn(b)
-            add_latents(b)
+        for r in range(per_half):
+            turn(per_half + r, low[r])
+            add_latents(per_half + r)
         quantize_z(1, 0, HALF)
-        quantize_wd(1, on_s)
-        project(1, 0, 0, HALF)
-        quantize_wd(2, on_s)
-        project(0, 1, 0, HALF)
-        project(0, 2, 0, HALF)
-        project(1, 1, 0, HALF)
-        store_scales(0)
-        project(1, 2, 0, HALF)
-        store_scales(1)
+        quantize_wd(1, (on_s, on_s))
+        units.append(project(1, 0, 0, HALF, high))
+        units.append(project(0, 1, 0, HALF, low))
+        quantize_wd(2, (on_v, on_v))
+        units.append(project(1, 1, 0, HALF, high))
+        units.append(project(0, 2, 0, HALF, low))
+        units.append(project(1, 2, 0, HALF, high))
+        for unit in units:
+            planes(unit)
+        store_scales(nc.scalar)

@@ -97,19 +97,16 @@ def tile_list_guided_latent_decode_kernel(
         wd_raw[2] = load_wd(2)
 
         v_w = [keep.tile([P, S], U32, name="v_w%d" % a, align_bytes=64) for a in range(passes)]
-        hcols = HALF // 16
-
-        def gather_words(a, h):
-            nc.vector.tensor_copy(
-                v_w[a][:, h * HALF : (h + 1) * HALF],
-                tab_w[a][:].bitcast(U32).indirect(offsets[:, h * hcols : (h + 1) * hcols]),
-            )
 
         v_s = [keep.tile([P, S], U8, name="v_s%d" % a, align_bytes=64) for a in range(passes)]
         for a in range(passes):
             nc.vector.tensor_copy(v_s[a][:], tab_s[:].bitcast(U8)[:, a * T : (a + 1) * T].indirect(offsets[:]))
-            for h in range(halves):
-                gather_words(a, h)
+            step = S if a == 0 else HALF
+            for c0 in range(0, S, step):
+                nc.vector.tensor_copy(
+                    v_w[a][:, c0 : c0 + step],
+                    tab_w[a][:].bitcast(U32).indirect(offsets[:, c0 // 16 : (c0 + step) // 16]),
+                )
 
         wc_q = []
         for a in range(passes):
@@ -124,12 +121,11 @@ def tile_list_guided_latent_decode_kernel(
             wc_q.append((codes, scales))
 
 
-        g_pick = [keep.tile([P, PACK, HALF], F32, name="g_pick%d" % h) for h in range(halves)]
+        g_pick = keep.tile([P, PACK, S], F32, name="g_pick")
 
-        def gather_g(t, h, c0=0, width=HALF):
-            first = (h * HALF + c0) // 16
+        def gather_g(t, c0, width):
             nc.vector.tensor_copy(
-                g_pick[h][:, t, c0 : c0 + width], g_tab[t][:].indirect(offsets[:, first : first + width // 16])
+                g_pick[:, t, c0 : c0 + width], g_tab[t][:].indirect(offsets[:, c0 // 16 : (c0 + width) // 16])
             )
 
         wu_s_bytes = wu_s[:].bitcast(U8)
@@ -179,7 +175,7 @@ def tile_list_guided_latent_decode_kernel(
             nc.vector.tensor_tensor(
                 z16[h][:, r * KP : (r + 1) * KP].rearrange("p (c i t) -> p c t i", i=2, t=PACK),
                 turned[b].rearrange("p t (c i) -> p c t i", i=2),
-                g_pick[h][:, :, r * P : (r + 1) * P].rearrange("p t (c i) -> p c t i", i=2),
+                g_pick[:, :, b * P : (b + 1) * P].rearrange("p t (c i) -> p c t i", i=2),
                 ADD,
             )
 
@@ -195,19 +191,18 @@ def tile_list_guided_latent_decode_kernel(
 
         wd_q = {}
 
-        def quantize_wd(g, copies):
+        def quantize_wd(g, copy):
             w16 = ring.tile([P, KP * PACK], BF16, name="w16", tag="w16", align_bytes=64)
-            for u, copy in enumerate(copies):
-                copy(
-                    w16[:].rearrange("p (u e m j) -> p u m j e", u=2, e=2, j=PACK)[:, u],
-                    wd_raw[g][:].rearrange("p j (m u e) -> p u m j e", u=2, e=2)[:, u],
-                )
+            copy(
+                w16[:].rearrange("p (u e m j) -> p u m j e", u=2, e=2, j=PACK),
+                wd_raw[g][:].rearrange("p j (m u e) -> p u m j e", u=2, e=2),
+            )
             codes = keep.tile([P, KP], U32, name="wd_c%d" % g, align_bytes=64)
             scales = keep.tile([P, KP], U8, name="wd_s%d" % g, align_bytes=64)
             nc.vector.quantize_mx(out=codes[:].bitcast(FP8X4), scales=scales[:], in_=w16[:])
             wd_q[g] = (codes, scales)
 
-        y_s = keep.tile([P, groups * S], U8, name="y_s", align_bytes=64)
+        y_s = [keep.tile([P, n * S], U8, name="y_s%d" % n, align_bytes=64) for n in (groups - 1, 1)]
         words32 = out_1.rearrange("g p m t -> g p (m t)").bitcast(I32)
         scales32 = out_2.bitcast(I32)
 
@@ -233,7 +228,7 @@ def tile_list_guided_latent_decode_kernel(
                 nc.scalar.copy(y[:, t0 : t0 + per_bank, :], bank)
                 t1 = t0 + per_bank
                 if t1 % step == 0:
-                    nc.sync.dma_start(rows[:, t1 - step : t1, :], y[:, t1 - step : t1, :])
+                    nc.scalar.dma_start(rows[:, t1 - step : t1, :], y[:, t1 - step : t1, :])
             return y, h, g, c0, width
 
         def planes(unit, weave=nc.vector.tensor_copy):
@@ -246,14 +241,16 @@ def tile_list_guided_latent_decode_kernel(
             )
             codes = ring.tile([P, width], U32, name="y_c", align_bytes=64, bufs=6)
             nc.vector.quantize_mx(
-                out=codes[:].bitcast(FP8X4), scales=y_s[:, g * S + cols.start : g * S + cols.stop], in_=y16[:]
+                out=codes[:].bitcast(FP8X4), scales=y_s[g // 2][:, g % 2 * S + cols.start : g % 2 * S + cols.stop], in_=y16[:]
             )
             nc.sync.dma_start(words32[g][:, cols], codes[:].bitcast(I32))
 
-        def store_scales(queue):
-            by_row = scales32.rearrange("g (q r) n -> r q g n", r=4)
+        def store_scales(g0, g1, queues):
+            by_row = scales32[g0:g1].rearrange("g (q r) n -> r q g n", r=4)
             for r in range(4):
-                queue.dma_start(by_row[r], y_s[r:P:32, :].bitcast(I32).rearrange("q (g n) -> q g n", g=groups))
+                queues[r % len(queues)].dma_start(
+                    by_row[r], y_s[g0 // 2][r:P:32, :].bitcast(I32).rearrange("q (g n) -> q g n", g=g1 - g0)
+                )
 
         quarter = HALF // 2
         on_s, on_v = nc.scalar.copy, nc.vector.tensor_copy
@@ -266,26 +263,28 @@ def tile_list_guided_latent_decode_kernel(
         for r in range(per_half):
             turn(r, low[r])
         for t in range(PACK - 1):
-            gather_g(t, 0)
-            gather_g(t, 1)
-        gather_g(PACK - 1, 0)
-        quantize_wd(0, (on_s, on_s))
+            gather_g(t, 0, S)
+        gather_g(PACK - 1, 0, HALF)
+        quantize_wd(0, on_s)
         for r in range(per_half):
             add_latents(r)
         quantize_z(0, 0, HALF)
-        units = [project(0, 0, 0, HALF, high, 1)]
-        gather_g(PACK - 1, 1)
+        units = [project(0, 0, 0, HALF, high, 2)]
+        gather_g(PACK - 1, HALF, HALF)
         for r in range(per_half):
             turn(per_half + r, low[r])
             add_latents(per_half + r)
         quantize_z(1, 0, HALF)
-        quantize_wd(1, (on_s, on_s))
-        units.append(project(1, 0, 0, HALF, high))
-        units.append(project(0, 1, 0, HALF, low))
-        quantize_wd(2, (on_v, on_v))
-        units.append(project(1, 1, 0, HALF, high))
-        units.append(project(0, 2, 0, HALF, low))
+        quantize_wd(1, on_s)
+        units.append(project(1, 0, 0, HALF, high, 4))
+        units.append(project(0, 1, 0, HALF, low, 4))
+        quantize_wd(2, on_v)
+        units.append(project(1, 1, 0, HALF, high, 4))
+        units.append(project(0, 2, 0, HALF, low, 4))
         units.append(project(1, 2, 0, HALF, high))
-        for unit in units:
+        for unit in units[:4]:
             planes(unit)
-        store_scales(nc.scalar)
+        store_scales(0, 2, [nc.sync])
+        for unit in units[4:]:
+            planes(unit)
+        store_scales(2, 3, [nc.scalar])

@@ -52,12 +52,12 @@ def tile_list_guided_latent_decode_kernel(
         make_identity(nc, ident[:])
 
         def load_table(a):
-            t = keep.tile([P, T], I32, name="tab_w%d" % a, align_bytes=64)
+            t = keep.tile([P, T], I32, name="tab_w%d" % a, tag="tab_w%d" % a, align_bytes=64)
             nc.sync.dma_start(t[:], tab_words[a].rearrange("p t i -> p (t i)").bitcast(I32))
             return t
 
         def load_wc(a):
-            t = ring.tile([P, PACK, H], F32, name="wc_raw%d" % a, tag="big", bufs=7)
+            t = keep.tile([P, PACK, H], F32, name="wc_raw%d" % a, tag="wc_raw%d" % a, align_bytes=64)
             nc.sync.dma_start(t[:], wc[a * KP : (a + 1) * KP, :].rearrange("(p j) c -> p j c", j=PACK))
             return t
 
@@ -67,7 +67,10 @@ def tile_list_guided_latent_decode_kernel(
             return x
 
         def load_wd(g):
-            x = ring.tile([P, PACK, KP], F32, name="wd_raw%d" % g, tag="big", bufs=7)
+            if g == 1:
+                x = keep.tile([P, PACK, KP], F32, name="wd_raw1", tag="wd_raw1")
+            else:
+                x = ring.tile([P, PACK, KP], F32, name="wd_raw%d" % g, tag="big", bufs=5)
             nc.sync.dma_start(x[:], wd[:, g * KP : (g + 1) * KP].rearrange("(p j) c -> p j c", j=PACK))
             return x
 
@@ -82,12 +85,12 @@ def tile_list_guided_latent_decode_kernel(
 
         tab_w, wc_raw, g_tab, wd_raw = {}, {}, {}, {}
         load_planes(tab_s, ts32)
+        nc.sync.dma_start(wu_w[:], wu_words.bitcast(I32).rearrange("a p n -> p a n"))
         tab_w[0] = load_table(0)
         wc_raw[0] = load_wc(0)
-        tab_w[1] = load_table(1)
         wc_raw[1] = load_wc(1)
+        tab_w[1] = load_table(1)
         load_planes(wu_s, us32)
-        nc.sync.dma_start(wu_w[:], wu_words.bitcast(I32).rearrange("a p n -> p a n"))
         g_tab[0] = load_g(0)
         g_tab[1] = load_g(1)
         g_tab[2] = load_g(2)
@@ -96,21 +99,27 @@ def tile_list_guided_latent_decode_kernel(
         wd_raw[1] = load_wd(1)
         wd_raw[2] = load_wd(2)
 
-        v_w = [keep.tile([P, S], U32, name="v_w%d" % a, align_bytes=64) for a in range(passes)]
+        v_w, v_s, wc_q = {}, {}, {}
 
-        v_s = [keep.tile([P, S], U8, name="v_s%d" % a, align_bytes=64) for a in range(passes)]
-        for a in range(passes):
-            nc.vector.tensor_copy(v_s[a][:], tab_s[:].bitcast(U8)[:, a * T : (a + 1) * T].indirect(offsets[:]))
-            step = S if a == 0 else HALF
-            for c0 in range(0, S, step):
-                nc.vector.tensor_copy(
-                    v_w[a][:, c0 : c0 + step],
-                    tab_w[a][:].bitcast(U32).indirect(offsets[:, c0 // 16 : (c0 + step) // 16]),
-                )
+        def gather_words(a, h0, h1, tag):
+            x = keep.tile([P, (h1 - h0) * HALF], U32, name="v_w", tag=tag, align_bytes=64)
+            nc.vector.tensor_copy(
+                x[:], tab_w[a][:].bitcast(U32).indirect(offsets[:, h0 * HALF // 16 : h1 * HALF // 16])
+            )
+            for h in range(h0, h1):
+                v_w[a, h] = x[:, (h - h0) * HALF : (h - h0 + 1) * HALF]
 
-        wc_q = []
-        for a in range(passes):
-            w16 = ring.tile([P, H * PACK], BF16, name="w16", tag="w16", align_bytes=64)
+        def gather_scales(a, h0, h1, tag):
+            x = keep.tile([P, (h1 - h0) * HALF], U8, name="v_s", tag=tag, align_bytes=64)
+            nc.vector.tensor_copy(
+                x[:],
+                tab_s[:].bitcast(U8)[:, a * T : (a + 1) * T].indirect(offsets[:, h0 * HALF // 16 : h1 * HALF // 16]),
+            )
+            for h in range(h0, h1):
+                v_s[a, h] = x[:, (h - h0) * HALF : (h - h0 + 1) * HALF]
+
+        def quantize_wc(a):
+            w16 = keep.tile([P, H * PACK], BF16, name="wc16", tag="wc16_%d" % a, align_bytes=64)
             nc.scalar.copy(
                 w16[:].rearrange("p (c i j) -> p c j i", i=2, j=PACK),
                 wc_raw[a][:].rearrange("p j (c i) -> p c j i", i=2),
@@ -118,14 +127,22 @@ def tile_list_guided_latent_decode_kernel(
             codes = keep.tile([P, H], U32, name="wc_c%d" % a, align_bytes=64)
             scales = keep.tile([P, H], U8, name="wc_s%d" % a, align_bytes=64)
             nc.vector.quantize_mx(out=codes[:].bitcast(FP8X4), scales=scales[:], in_=w16[:])
-            wc_q.append((codes, scales))
+            wc_q[a] = (codes, scales)
 
+        gather_scales(0, 0, 2, "v_s0")
+        gather_words(0, 0, 2, "v_w0")
+        gather_scales(1, 0, 2, "tab_w0")
+        quantize_wc(0)
+        gather_words(1, 0, 1, "v_w1")
+        quantize_wc(1)
+        gather_words(1, 1, 2, "wc_raw1")
 
-        g_pick = keep.tile([P, PACK, S], F32, name="g_pick")
+        g_pick = keep.tile([P, 2 * PACK + 1, HALF], F32, name="g_pick", align_bytes=64)
+        g_first = [0, PACK]
 
-        def gather_g(t, c0, width):
+        def gather_g(t, h):
             nc.vector.tensor_copy(
-                g_pick[:, t, c0 : c0 + width], g_tab[t][:].indirect(offsets[:, c0 // 16 : (c0 + width) // 16])
+                g_pick[:, g_first[h] + t, :], g_tab[t][:].indirect(offsets[:, h * HALF // 16 : (h + 1) * HALF // 16])
             )
 
         wu_s_bytes = wu_s[:].bitcast(U8)
@@ -134,17 +151,17 @@ def tile_list_guided_latent_decode_kernel(
         banks = [psum.tile([P, BANK], F32, name="bank%d" % i) for i in range(8)]
 
         def predict(b, which, bank):
-            cols = slice(b * P, (b + 1) * P)
-            order = range(passes) if which == "b" else range(passes - 1, -1, -1)
-            for i, a in enumerate(order):
+            h, r = divmod(b, per_half)
+            cols = slice(r * P, (r + 1) * P)
+            for i, a in enumerate(range(passes)):
                 if which == "b":
                     rhs, rhs_scale = wu_w[:, a, :].bitcast(FP4X4), wu_s_bytes[:, a * H : (a + 1) * H]
                 else:
                     rhs, rhs_scale = wc_q[a][0][:].bitcast(FP8X4), wc_q[a][1][:]
                 nc.tensor.matmul_mx(
                     out=bank[:],
-                    lhsT=v_w[a][:, cols].bitcast(FP8X4),
-                    lhsT_scale=v_s[a][:, cols],
+                    lhsT=v_w[a, h][:, cols].bitcast(FP8X4),
+                    lhsT_scale=v_s[a, h][:, cols],
                     rhs=rhs,
                     rhs_scale=rhs_scale,
                     start=(i == 0),
@@ -168,21 +185,24 @@ def tile_list_guided_latent_decode_kernel(
                     nc.tensor.matmul(u[:, t, :], x[:, t, :], ident[:], start=(i == 0), stop=(i == 1), is_transpose=True)
             turned[b] = u
 
-        z16 = [keep.tile([P, HALF * PACK], BF16, name="z16_%d" % h, align_bytes=64) for h in range(halves)]
+        z16 = {}
 
         def add_latents(b):
             h, r = divmod(b, per_half)
+            if r == 0:
+                z16[h] = keep.tile([P, HALF * PACK], BF16, name="z16", tag=["z16", "wc16_1"][h], align_bytes=64)
             nc.vector.tensor_tensor(
                 z16[h][:, r * KP : (r + 1) * KP].rearrange("p (c i t) -> p c t i", i=2, t=PACK),
                 turned[b].rearrange("p t (c i) -> p c t i", i=2),
-                g_pick[:, :, b * P : (b + 1) * P].rearrange("p t (c i) -> p c t i", i=2),
+                g_pick[:, g_first[h] : g_first[h] + PACK, r * P : (r + 1) * P].rearrange("p t (c i) -> p c t i", i=2),
                 ADD,
             )
 
-        z_c = [keep.tile([P, HALF], U32, name="z_c%d" % h, align_bytes=64) for h in range(halves)]
+        z_c = {}
         z_s = [keep.tile([P, HALF], U8, name="z_s%d" % h, align_bytes=64) for h in range(halves)]
 
         def quantize_z(h, c0, width):
+            z_c[h] = keep.tile([P, HALF], U32, name="z_c", tag=["z_c", "wc16_0"][h], align_bytes=64)
             nc.vector.quantize_mx(
                 out=z_c[h][:, c0 : c0 + width].bitcast(FP8X4),
                 scales=z_s[h][:, c0 : c0 + width],
@@ -192,24 +212,32 @@ def tile_list_guided_latent_decode_kernel(
         wd_q = {}
 
         def quantize_wd(g, copy):
-            w16 = ring.tile([P, KP * PACK], BF16, name="w16", tag="w16", align_bytes=64)
+            if g == 0:
+                w16 = g_pick[:, 2 * PACK - 1 :, :].rearrange("p a c -> p (a c)").bitcast(BF16)
+            elif g == 1:
+                w16 = keep.tile([P, KP * PACK], BF16, name="w16", tag="wc16_0", align_bytes=64)[:]
+            else:
+                w16 = ring.tile([P, KP * PACK], BF16, name="w16", tag="h16", align_bytes=64, bufs=3)[:]
             copy(
-                w16[:].rearrange("p (u e m j) -> p u m j e", u=2, e=2, j=PACK),
+                w16.rearrange("p (u e m j) -> p u m j e", u=2, e=2, j=PACK),
                 wd_raw[g][:].rearrange("p j (m u e) -> p u m j e", u=2, e=2),
             )
             codes = keep.tile([P, KP], U32, name="wd_c%d" % g, align_bytes=64)
             scales = keep.tile([P, KP], U8, name="wd_s%d" % g, align_bytes=64)
-            nc.vector.quantize_mx(out=codes[:].bitcast(FP8X4), scales=scales[:], in_=w16[:])
+            nc.vector.quantize_mx(out=codes[:].bitcast(FP8X4), scales=scales[:], in_=w16)
             wd_q[g] = (codes, scales)
 
-        y_s = [keep.tile([P, n * S], U8, name="y_s%d" % n, align_bytes=64) for n in (groups - 1, 1)]
+        y_s = keep.tile([P, groups * S], U8, name="y_s", align_bytes=64)
         words32 = out_1.rearrange("g p m t -> g p (m t)").bitcast(I32)
         scales32 = out_2.bitcast(I32)
 
         def project(h, g, c0, width, free, step=2):
             local = slice(c0, c0 + width)
             cols = slice(h * HALF + c0, h * HALF + c0 + width)
-            y = ring.tile([P, PACK, width], F32, name="y", tag="big", bufs=7)
+            if (h, g) == (0, 0):
+                y = keep.tile([P, PACK, width], F32, name="y", tag="wd_raw1")
+            else:
+                y = ring.tile([P, PACK, width], F32, name="y", tag="big", bufs=5)
             rows = out_0[g * KP : (g + 1) * KP, cols].rearrange("(p t) s -> p t s", t=PACK)
             per_bank = BANK // width
             for t0 in range(0, PACK, per_bank):
@@ -231,17 +259,21 @@ def tile_list_guided_latent_decode_kernel(
                     nc.scalar.dma_start(rows[:, t1 - step : t1, :], y[:, t1 - step : t1, :])
             return y, h, g, c0, width
 
-        def planes(unit, weave=nc.vector.tensor_copy):
+        def weave(unit):
             y, h, g, c0, width = unit
-            cols = slice(h * HALF + c0, h * HALF + c0 + width)
-            y16 = ring.tile([P, width * PACK], BF16, name="y16", align_bytes=64)
-            weave(
+            y16 = ring.tile([P, width * PACK], BF16, name="y16", tag="h16", align_bytes=64, bufs=3)
+            nc.vector.tensor_copy(
                 y16[:].rearrange("p (c i t) -> p c t i", i=2, t=PACK),
                 y[:].rearrange("p t (c i) -> p c t i", i=2),
             )
+            return y16
+
+        def planes(unit, y16):
+            y, h, g, c0, width = unit
+            cols = slice(h * HALF + c0, h * HALF + c0 + width)
             codes = ring.tile([P, width], U32, name="y_c", align_bytes=64, bufs=6)
             nc.vector.quantize_mx(
-                out=codes[:].bitcast(FP8X4), scales=y_s[g // 2][:, g % 2 * S + cols.start : g % 2 * S + cols.stop], in_=y16[:]
+                out=codes[:].bitcast(FP8X4), scales=y_s[:, g * S + cols.start : g * S + cols.stop], in_=y16[:]
             )
             nc.sync.dma_start(words32[g][:, cols], codes[:].bitcast(I32))
 
@@ -249,42 +281,39 @@ def tile_list_guided_latent_decode_kernel(
             by_row = scales32[g0:g1].rearrange("g (q r) n -> r q g n", r=4)
             for r in range(4):
                 queues[r % len(queues)].dma_start(
-                    by_row[r], y_s[g0 // 2][r:P:32, :].bitcast(I32).rearrange("q (g n) -> q g n", g=g1 - g0)
+                    by_row[r], y_s[r:P:32, :].bitcast(I32).rearrange("q (g n) -> q g n", g=g1 - g0)
                 )
 
-        quarter = HALF // 2
         on_s, on_v = nc.scalar.copy, nc.vector.tensor_copy
         low, high = banks[:4], banks[4:]
-        for h in range(halves):
-            for r in range(per_half):
-                predict(h * per_half + r, "b", low[r])
-            for r in range(per_half):
-                predict(h * per_half + r, "a", high[r])
-        for r in range(per_half):
-            turn(r, low[r])
+        for b in range(blocks):
+            predict(b, "a", banks[2 * b % 8])
+            predict(b, "b", banks[(2 * b + 1) % 8])
+        for b in range(blocks):
+            turn(b, banks[b])
         for t in range(PACK - 1):
-            gather_g(t, 0, S)
-        gather_g(PACK - 1, 0, HALF)
-        quantize_wd(0, on_s)
+            gather_g(t, 0)
+            gather_g(t, 1)
+        gather_g(PACK - 1, 0)
         for r in range(per_half):
             add_latents(r)
+        quantize_wd(0, on_s)
         quantize_z(0, 0, HALF)
-        units = [project(0, 0, 0, HALF, high, 2)]
-        gather_g(PACK - 1, HALF, HALF)
+        gather_g(PACK - 1, 1)
         for r in range(per_half):
-            turn(per_half + r, low[r])
             add_latents(per_half + r)
-        quantize_z(1, 0, HALF)
         quantize_wd(1, on_s)
-        units.append(project(1, 0, 0, HALF, high, 4))
-        units.append(project(0, 1, 0, HALF, low, 4))
+        units = [project(0, 0, 0, HALF, low, 2)]
+        units.append(project(0, 1, 0, HALF, low, 2))
+        quantize_z(1, 0, HALF)
+        units.append(project(1, 0, 0, HALF, high, 2))
         quantize_wd(2, on_v)
-        units.append(project(1, 1, 0, HALF, high, 4))
-        units.append(project(0, 2, 0, HALF, low, 4))
-        units.append(project(1, 2, 0, HALF, high))
-        for unit in units[:4]:
-            planes(unit)
-        store_scales(0, 2, [nc.sync])
-        for unit in units[4:]:
-            planes(unit)
-        store_scales(2, 3, [nc.scalar])
+        units.append(project(1, 1, 0, HALF, low, 2))
+        units.append(project(0, 2, 0, HALF, high, 2))
+        units.append(project(1, 2, 0, HALF, low, 2))
+        woven = [weave(units[0])]
+        for i, unit in enumerate(units):
+            if i + 1 < len(units):
+                woven.append(weave(units[i + 1]))
+            planes(unit, woven[i])
+        store_scales(0, groups, [nc.scalar, nc.sync])

@@ -190,7 +190,7 @@ def tile_list_guided_latent_decode_kernel(
         def add_latents(b):
             h, r = divmod(b, per_half)
             if r == 0:
-                z16[h] = keep.tile([P, HALF * PACK], BF16, name="z16", tag=["z16", "wc16_1"][h], align_bytes=64)
+                z16[h] = keep.tile([P, HALF * PACK], BF16, name="z16", tag=["wc16_1", "wc16_0"][h], align_bytes=64)
             nc.vector.tensor_tensor(
                 z16[h][:, r * KP : (r + 1) * KP].rearrange("p (c i t) -> p c t i", i=2, t=PACK),
                 turned[b].rearrange("p t (c i) -> p c t i", i=2),
@@ -202,7 +202,7 @@ def tile_list_guided_latent_decode_kernel(
         z_s = [keep.tile([P, HALF], U8, name="z_s%d" % h, align_bytes=64) for h in range(halves)]
 
         def quantize_z(h, c0, width):
-            z_c[h] = keep.tile([P, HALF], U32, name="z_c", tag=["z_c", "wc16_0"][h], align_bytes=64)
+            z_c[h] = keep.tile([P, HALF], U32, name="z_c", tag="z_c%d" % h, align_bytes=64)
             nc.vector.quantize_mx(
                 out=z_c[h][:, c0 : c0 + width].bitcast(FP8X4),
                 scales=z_s[h][:, c0 : c0 + width],
@@ -300,9 +300,9 @@ def tile_list_guided_latent_decode_kernel(
         quantize_wd(0, on_s)
         quantize_z(0, 0, HALF)
         gather_g(PACK - 1, 1)
+        quantize_wd(1, on_s)
         for r in range(per_half):
             add_latents(per_half + r)
-        quantize_wd(1, on_s)
         units = [project(0, 0, 0, HALF, low, 2)]
         units.append(project(0, 1, 0, HALF, low, 2))
         quantize_z(1, 0, HALF)

@@ -23,6 +23,7 @@ KP = P * PACK
 BANK = 512
 HALF = 512
 QUADS = 4
+SPLIT = 256
 
 
 def tile_list_guided_latent_decode_kernel(
@@ -66,17 +67,18 @@ def tile_list_guided_latent_decode_kernel(
             nc.sync.dma_start(x[:], gT.rearrange("(p t) c -> p t c", t=PACK)[:, t, :])
             return x
 
-        def load_wd(g):
-            if g == 1:
-                x = keep.tile([P, PACK, KP], F32, name="wd_raw1", tag="wd_raw1")
+        def load_wd(g0, g1):
+            if g0 == 1:
+                x = keep.tile([P, PACK, KP], F32, name="wd_raw", tag="wd_raw1")
             else:
-                x = ring.tile([P, PACK, KP], F32, name="wd_raw%d" % g, tag="big", bufs=5)
-            nc.sync.dma_start(x[:], wd[:, g * KP : (g + 1) * KP].rearrange("(p j) c -> p j c", j=PACK))
-            return x
+                x = ring.tile([P, PACK, KP], F32, name="wd_raw", tag="big", bufs=4)
+            nc.sync.dma_start(x[:], wd[:, g0 * KP : g1 * KP].rearrange("(p j) c -> p j c", j=PACK))
+            for g in range(g0, g1):
+                wd_raw[g] = x[:, :, (g - g0) * KP : (g - g0 + 1) * KP]
 
         ts32 = tab_scales.bitcast(I32)
         us32 = wu_scales.bitcast(I32)
-        wu_w = keep.tile([P, passes, 2 * H // 4], I32, name="wu_w", align_bytes=64)
+        wu_w = [keep.tile([P, 2 * H // 4], I32, name="wu_w%d" % a, align_bytes=64) for a in range(passes)]
 
         def load_planes(tile, rows):
             by_row = rows.rearrange("a (q r) n -> r q a n", r=4)
@@ -85,19 +87,20 @@ def tile_list_guided_latent_decode_kernel(
 
         tab_w, wc_raw, g_tab, wd_raw = {}, {}, {}, {}
         load_planes(tab_s, ts32)
-        nc.sync.dma_start(wu_w[:], wu_words.bitcast(I32).rearrange("a p n -> p a n"))
+        nc.sync.dma_start(wu_w[0][:], wu_words[0].bitcast(I32))
         tab_w[0] = load_table(0)
         wc_raw[0] = load_wc(0)
         wc_raw[1] = load_wc(1)
         tab_w[1] = load_table(1)
         load_planes(wu_s, us32)
+        nc.sync.dma_start(wu_w[1][:], wu_words[1].bitcast(I32))
         g_tab[0] = load_g(0)
         g_tab[1] = load_g(1)
         g_tab[2] = load_g(2)
         g_tab[3] = load_g(3)
-        wd_raw[0] = load_wd(0)
-        wd_raw[1] = load_wd(1)
-        wd_raw[2] = load_wd(2)
+        load_wd(0, 1)
+        load_wd(1, 2)
+        load_wd(2, 3)
 
         v_w, v_s, wc_q = {}, {}, {}
 
@@ -137,12 +140,13 @@ def tile_list_guided_latent_decode_kernel(
         quantize_wc(1)
         gather_words(1, 1, 2, "wc_raw1")
 
-        g_pick = keep.tile([P, 2 * PACK + 1, HALF], F32, name="g_pick", align_bytes=64)
-        g_first = [0, PACK]
+        g_flat = keep.tile([P, PACK * S + HALF], F32, name="g_flat", align_bytes=64)
+        g_pick = g_flat[:, : PACK * S].rearrange("p (t s) -> p t s", t=PACK)
 
-        def gather_g(t, h):
+        def gather_g(t, h0, h1):
             nc.vector.tensor_copy(
-                g_pick[:, g_first[h] + t, :], g_tab[t][:].indirect(offsets[:, h * HALF // 16 : (h + 1) * HALF // 16])
+                g_flat[:, t * S + h0 * HALF : t * S + h1 * HALF],
+                g_tab[t][:].indirect(offsets[:, h0 * HALF // 16 : h1 * HALF // 16]),
             )
 
         wu_s_bytes = wu_s[:].bitcast(U8)
@@ -155,7 +159,7 @@ def tile_list_guided_latent_decode_kernel(
             cols = slice(r * P, (r + 1) * P)
             for i, a in enumerate(range(passes)):
                 if which == "b":
-                    rhs, rhs_scale = wu_w[:, a, :].bitcast(FP4X4), wu_s_bytes[:, a * H : (a + 1) * H]
+                    rhs, rhs_scale = wu_w[a][:].bitcast(FP4X4), wu_s_bytes[:, a * H : (a + 1) * H]
                 else:
                     rhs, rhs_scale = wc_q[a][0][:].bitcast(FP8X4), wc_q[a][1][:]
                 nc.tensor.matmul_mx(
@@ -194,7 +198,7 @@ def tile_list_guided_latent_decode_kernel(
             nc.vector.tensor_tensor(
                 z16[h][:, r * KP : (r + 1) * KP].rearrange("p (c i t) -> p c t i", i=2, t=PACK),
                 turned[b].rearrange("p t (c i) -> p c t i", i=2),
-                g_pick[:, g_first[h] : g_first[h] + PACK, r * P : (r + 1) * P].rearrange("p t (c i) -> p c t i", i=2),
+                g_pick[:, :, b * P : (b + 1) * P].rearrange("p t (c i) -> p c t i", i=2),
                 ADD,
             )
 
@@ -209,73 +213,78 @@ def tile_list_guided_latent_decode_kernel(
                 in_=z16[h][:, PACK * c0 : PACK * (c0 + width)],
             )
 
-        wd_q = {}
-
-        def quantize_wd(g, copy):
-            if g == 0:
-                w16 = g_pick[:, 2 * PACK - 1 :, :].rearrange("p a c -> p (a c)").bitcast(BF16)
-            elif g == 1:
-                w16 = keep.tile([P, KP * PACK], BF16, name="w16", tag="wc16_0", align_bytes=64)[:]
-            else:
-                w16 = ring.tile([P, KP * PACK], BF16, name="w16", tag="h16", align_bytes=64, bufs=3)[:]
-            copy(
-                w16.rearrange("p (u e m j) -> p u m j e", u=2, e=2, j=PACK),
-                wd_raw[g][:].rearrange("p j (m u e) -> p u m j e", u=2, e=2),
+        wd_q = [
+            (
+                keep.tile([P, KP], U32, name="wd_c%d" % g, align_bytes=64),
+                keep.tile([P, KP], U8, name="wd_s%d" % g, align_bytes=64),
             )
-            codes = keep.tile([P, KP], U32, name="wd_c%d" % g, align_bytes=64)
-            scales = keep.tile([P, KP], U8, name="wd_s%d" % g, align_bytes=64)
-            nc.vector.quantize_mx(out=codes[:].bitcast(FP8X4), scales=scales[:], in_=w16)
-            wd_q[g] = (codes, scales)
+            for g in range(groups)
+        ]
+
+        def quantize_wd(g, u0, u1, w16, copy):
+            copy(
+                w16.rearrange("p (u e m j) -> p u m j e", e=2, m=P, j=PACK),
+                wd_raw[g].rearrange("p j (m u e) -> p u m j e", u=2, e=2)[:, u0:u1],
+            )
+            cols = slice(2 * P * u0, 2 * P * u1)
+            nc.vector.quantize_mx(out=wd_q[g][0][:, cols].bitcast(FP8X4), scales=wd_q[g][1][:, cols], in_=w16)
 
         y_s = keep.tile([P, groups * S], U8, name="y_s", align_bytes=64)
         words32 = out_1.rearrange("g p m t -> g p (m t)").bitcast(I32)
         scales32 = out_2.bitcast(I32)
 
-        def project(h, g, c0, width, free, step=2):
-            local = slice(c0, c0 + width)
-            cols = slice(h * HALF + c0, h * HALF + c0 + width)
-            if (h, g) == (0, 0):
-                y = keep.tile([P, PACK, width], F32, name="y", tag="wd_raw1")
-            else:
-                y = ring.tile([P, PACK, width], F32, name="y", tag="big", bufs=5)
-            rows = out_0[g * KP : (g + 1) * KP, cols].rearrange("(p t) s -> p t s", t=PACK)
-            per_bank = BANK // width
-            for t0 in range(0, PACK, per_bank):
-                bank = free[t0 // per_bank][:].rearrange("p (j s) -> p j s", j=per_bank)
-                for j in range(per_bank):
-                    wcols = slice((t0 + j) * P, (t0 + j + 1) * P)
-                    nc.tensor.matmul_mx(
-                        out=bank[:, j, :],
-                        lhsT=wd_q[g][0][:, wcols].bitcast(FP8X4),
-                        lhsT_scale=wd_q[g][1][:, wcols],
-                        rhs=z_c[h][:, local].bitcast(FP8X4),
-                        rhs_scale=z_s[h][:, local],
-                        start=True,
-                        stop=True,
-                    )
-                nc.scalar.copy(y[:, t0 : t0 + per_bank, :], bank)
-                t1 = t0 + per_bank
-                if t1 % step == 0:
-                    nc.scalar.dma_start(rows[:, t1 - step : t1, :], y[:, t1 - step : t1, :])
-            return y, h, g, c0, width
+        def project(h, g, t, bank, y):
+            wcols = slice(t * P, (t + 1) * P)
+            nc.tensor.matmul_mx(
+                out=bank[:],
+                lhsT=wd_q[g][0][:, wcols].bitcast(FP8X4),
+                lhsT_scale=wd_q[g][1][:, wcols],
+                rhs=z_c[h][:].bitcast(FP8X4),
+                rhs_scale=z_s[h][:],
+                start=True,
+                stop=True,
+            )
+            nc.scalar.copy(y[:, t, :], bank[:])
 
-        def weave(unit):
-            y, h, g, c0, width = unit
-            y16 = ring.tile([P, width * PACK], BF16, name="y16", tag="h16", align_bytes=64, bufs=3)
-            nc.vector.tensor_copy(
-                y16[:].rearrange("p (c i t) -> p c t i", i=2, t=PACK),
-                y[:].rearrange("p t (c i) -> p c t i", i=2),
+        def rows(g):
+            return out_0[g * KP : (g + 1) * KP, :].rearrange("(p t) s -> p t s", t=PACK)
+
+        def project_half(h, g, free, y):
+            for t in range(PACK):
+                project(h, g, t, free[t], y)
+                if t % 2:
+                    nc.scalar.dma_start(rows(g)[:, t - 1 : t + 1, h * HALF : (h + 1) * HALF], y[:, t - 1 : t + 1, :])
+            return y
+
+        def project_group(g, y):
+            parts = [y[:, :, h * HALF : (h + 1) * HALF] for h in range(halves)]
+            for u in range(2):
+                for h in range(halves):
+                    for e in range(2):
+                        project(h, g, 2 * u + e, banks[4 * (1 - u) + 2 * h + e], parts[h])
+                nc.scalar.dma_start(rows(g)[:, 2 * u : 2 * u + 2, :], y[:, 2 * u : 2 * u + 2, :])
+            return parts
+
+        def weave(y, y16, copy):
+            copy(
+                y16.rearrange("p (c i t) -> p c t i", i=2, t=PACK),
+                y.rearrange("p t (c i) -> p c t i", i=2),
             )
             return y16
 
-        def planes(unit, y16):
-            y, h, g, c0, width = unit
-            cols = slice(h * HALF + c0, h * HALF + c0 + width)
-            codes = ring.tile([P, width], U32, name="y_c", align_bytes=64, bufs=6)
+        y_c = [keep.tile([P, S], U32, name="y_c%d" % g, align_bytes=64) for g in range(groups)]
+
+        def planes(g, h, y16):
+            c0 = h * HALF
             nc.vector.quantize_mx(
-                out=codes[:].bitcast(FP8X4), scales=y_s[:, g * S + cols.start : g * S + cols.stop], in_=y16[:]
+                out=y_c[g][:, c0 : c0 + HALF].bitcast(FP8X4),
+                scales=y_s[:, g * S + c0 : g * S + c0 + HALF],
+                in_=y16,
             )
-            nc.sync.dma_start(words32[g][:, cols], codes[:].bitcast(I32))
+            if g == groups - 1:
+                nc.sync.dma_start(words32[g][:, c0 : c0 + HALF], y_c[g][:, c0 : c0 + HALF].bitcast(I32))
+            elif h == halves - 1:
+                nc.sync.dma_start(words32[g], y_c[g][:].bitcast(I32))
 
         def store_scales(g0, g1, queues):
             by_row = scales32[g0:g1].rearrange("g (q r) n -> r q g n", r=4)
@@ -283,6 +292,11 @@ def tile_list_guided_latent_decode_kernel(
                 queues[r % len(queues)].dma_start(
                     by_row[r], y_s[r:P:32, :].bitcast(I32).rearrange("q (g n) -> q g n", g=g1 - g0)
                 )
+
+        def half16(name, tag):
+            if tag == "h16":
+                return ring.tile([P, HALF * PACK], BF16, name=name, tag=tag, align_bytes=64, bufs=3)
+            return keep.tile([P, HALF * PACK], BF16, name=name, tag=tag, align_bytes=64)
 
         on_s, on_v = nc.scalar.copy, nc.vector.tensor_copy
         low, high = banks[:4], banks[4:]
@@ -292,28 +306,36 @@ def tile_list_guided_latent_decode_kernel(
         for b in range(blocks):
             turn(b, banks[b])
         for t in range(PACK - 1):
-            gather_g(t, 0)
-            gather_g(t, 1)
-        gather_g(PACK - 1, 0)
+            gather_g(t, 0, 2)
+        gather_g(PACK - 1, 0, 1)
         for r in range(per_half):
             add_latents(r)
-        quantize_wd(0, on_s)
+        quantize_wd(0, 0, 2, g_flat[:, PACK * S - HALF :].bitcast(BF16), on_s)
         quantize_z(0, 0, HALF)
-        gather_g(PACK - 1, 1)
-        quantize_wd(1, on_s)
+        gather_g(PACK - 1, 1, 2)
+        quantize_wd(1, 0, 2, half16("wd16", "wc16_0")[:], on_s)
         for r in range(per_half):
             add_latents(per_half + r)
-        units = [project(0, 0, 0, HALF, low, 2)]
-        units.append(project(0, 1, 0, HALF, low, 2))
+
+        def y_tile():
+            return ring.tile([P, PACK, HALF], F32, name="y", tag="big", bufs=4)[:]
+
+        y00 = keep.tile([P, PACK, HALF], F32, name="y00", tag="wd_raw1")
+        units = [project_half(0, 0, low, y00[:]), project_half(0, 1, low, y_tile())]
         quantize_z(1, 0, HALF)
-        units.append(project(1, 0, 0, HALF, high, 2))
-        quantize_wd(2, on_v)
-        units.append(project(1, 1, 0, HALF, low, 2))
-        units.append(project(0, 2, 0, HALF, high, 2))
-        units.append(project(1, 2, 0, HALF, low, 2))
-        woven = [weave(units[0])]
-        for i, unit in enumerate(units):
-            if i + 1 < len(units):
-                woven.append(weave(units[i + 1]))
-            planes(unit, woven[i])
+        units.append(project_half(1, 0, high, y_tile()))
+        quantize_wd(2, 0, 2, half16("wd16", "h16")[:], on_v)
+        units.append(project_half(1, 1, low, y_tile()))
+        units.extend(project_group(2, g_pick))
+        order = [(0, 0), (0, 1), (1, 0), (1, 1), (0, 2), (1, 2)]
+        woven = [weave(units[0], half16("y16", "h16")[:], on_v)]
+        for i, (h, g) in enumerate(order):
+            if i + 2 < len(order):
+                woven.append(weave(units[i + 1], half16("y16", "h16")[:], on_v))
+            elif i + 1 < len(order):
+                y16 = half16("y16", "h16")[:]
+                weave(units[i + 1][:, :, :SPLIT], y16[:, : PACK * SPLIT], on_v)
+                weave(units[i + 1][:, :, SPLIT:], y16[:, PACK * SPLIT :], on_s)
+                woven.append(y16)
+            planes(g, h, woven[i])
         store_scales(0, groups, [nc.scalar, nc.sync])

@@ -143,10 +143,9 @@ def tile_list_guided_latent_decode_kernel(
         g_flat = keep.tile([P, PACK * S + HALF], F32, name="g_flat", align_bytes=64)
         g_pick = g_flat[:, : PACK * S].rearrange("p (t s) -> p t s", t=PACK)
 
-        def gather_g(t, h0, h1):
+        def gather_g(t, c0, c1):
             nc.vector.tensor_copy(
-                g_flat[:, t * S + h0 * HALF : t * S + h1 * HALF],
-                g_tab[t][:].indirect(offsets[:, h0 * HALF // 16 : h1 * HALF // 16]),
+                g_flat[:, t * S + c0 : t * S + c1], g_tab[t][:].indirect(offsets[:, c0 // 16 : c1 // 16])
             )
 
         wu_s_bytes = wu_s[:].bitcast(U8)
@@ -205,13 +204,18 @@ def tile_list_guided_latent_decode_kernel(
         z_c = {}
         z_s = [keep.tile([P, HALF], U8, name="z_s%d" % h, align_bytes=64) for h in range(halves)]
 
-        def quantize_z(h, c0, width):
+        def quantize(codes, scales, x16):
+            width = codes.shape[1] // 2
+            for c0 in (0, width):
+                nc.vector.quantize_mx(
+                    out=codes[:, c0 : c0 + width].bitcast(FP8X4),
+                    scales=scales[:, c0 : c0 + width],
+                    in_=x16[:, PACK * c0 : PACK * (c0 + width)],
+                )
+
+        def quantize_z(h):
             z_c[h] = keep.tile([P, HALF], U32, name="z_c", tag="z_c%d" % h, align_bytes=64)
-            nc.vector.quantize_mx(
-                out=z_c[h][:, c0 : c0 + width].bitcast(FP8X4),
-                scales=z_s[h][:, c0 : c0 + width],
-                in_=z16[h][:, PACK * c0 : PACK * (c0 + width)],
-            )
+            quantize(z_c[h][:], z_s[h][:], z16[h][:])
 
         wd_q = [
             (
@@ -221,11 +225,14 @@ def tile_list_guided_latent_decode_kernel(
             for g in range(groups)
         ]
 
-        def quantize_wd(g, u0, u1, w16, copy):
+        def round_wd(g, u0, u1, w16, copy):
             copy(
                 w16.rearrange("p (u e m j) -> p u m j e", e=2, m=P, j=PACK),
                 wd_raw[g].rearrange("p j (m u e) -> p u m j e", u=2, e=2)[:, u0:u1],
             )
+
+        def quantize_wd(g, u0, u1, w16, copy):
+            round_wd(g, u0, u1, w16, copy)
             cols = slice(2 * P * u0, 2 * P * u1)
             nc.vector.quantize_mx(out=wd_q[g][0][:, cols].bitcast(FP8X4), scales=wd_q[g][1][:, cols], in_=w16)
 
@@ -276,11 +283,7 @@ def tile_list_guided_latent_decode_kernel(
 
         def planes(g, h, y16):
             c0 = h * HALF
-            nc.vector.quantize_mx(
-                out=y_c[g][:, c0 : c0 + HALF].bitcast(FP8X4),
-                scales=y_s[:, g * S + c0 : g * S + c0 + HALF],
-                in_=y16,
-            )
+            quantize(y_c[g][:, c0 : c0 + HALF], y_s[:, g * S + c0 : g * S + c0 + HALF], y16)
             if g == groups - 1:
                 nc.sync.dma_start(words32[g][:, c0 : c0 + HALF], y_c[g][:, c0 : c0 + HALF].bitcast(I32))
             elif h == halves - 1:
@@ -306,13 +309,14 @@ def tile_list_guided_latent_decode_kernel(
         for b in range(blocks):
             turn(b, banks[b])
         for t in range(PACK - 1):
-            gather_g(t, 0, 2)
-        gather_g(PACK - 1, 0, 1)
+            gather_g(t, 0, S)
+        gather_g(PACK - 1, 0, HALF // 2)
+        gather_g(PACK - 1, HALF // 2, HALF)
         for r in range(per_half):
             add_latents(r)
         quantize_wd(0, 0, 2, g_flat[:, PACK * S - HALF :].bitcast(BF16), on_s)
-        quantize_z(0, 0, HALF)
-        gather_g(PACK - 1, 1, 2)
+        quantize_z(0)
+        gather_g(PACK - 1, HALF, S)
         quantize_wd(1, 0, 2, half16("wd16", "wc16_0")[:], on_s)
         for r in range(per_half):
             add_latents(per_half + r)
@@ -322,20 +326,18 @@ def tile_list_guided_latent_decode_kernel(
 
         y00 = keep.tile([P, PACK, HALF], F32, name="y00", tag="wd_raw1")
         units = [project_half(0, 0, low, y00[:]), project_half(0, 1, low, y_tile())]
-        quantize_z(1, 0, HALF)
+        quantize_z(1)
         units.append(project_half(1, 0, high, y_tile()))
-        quantize_wd(2, 0, 2, half16("wd16", "h16")[:], on_v)
+        wd16 = half16("wd16", "h16")
+        for u in range(2):
+            round_wd(2, u, u + 1, wd16[:, 2 * KP * u : 2 * KP * (u + 1)], on_v)
+        quantize(wd_q[2][0][:], wd_q[2][1][:], wd16[:])
         units.append(project_half(1, 1, low, y_tile()))
         units.extend(project_group(2, g_pick))
         order = [(0, 0), (0, 1), (1, 0), (1, 1), (0, 2), (1, 2)]
-        woven = [weave(units[0], half16("y16", "h16")[:], on_v)]
         for i, (h, g) in enumerate(order):
-            if i + 2 < len(order):
-                woven.append(weave(units[i + 1], half16("y16", "h16")[:], on_v))
-            elif i + 1 < len(order):
-                y16 = half16("y16", "h16")[:]
-                weave(units[i + 1][:, :, :SPLIT], y16[:, : PACK * SPLIT], on_v)
-                weave(units[i + 1][:, :, SPLIT:], y16[:, PACK * SPLIT :], on_s)
-                woven.append(y16)
-            planes(g, h, woven[i])
+            y16 = half16("y16", "h16")[:]
+            weave(units[i][:, :, :SPLIT], y16[:, : PACK * SPLIT], on_v)
+            weave(units[i][:, :, SPLIT:], y16[:, PACK * SPLIT :], on_s if i + 1 == len(order) else on_v)
+            planes(g, h, y16)
         store_scales(0, groups, [nc.scalar, nc.sync])

@@ -24,6 +24,8 @@ BANK = 512
 HALF = 512
 QUADS = 4
 SPLIT = 256
+LAST = 256
+SHARE = 96
 
 
 def tile_list_guided_latent_decode_kernel(
@@ -225,10 +227,10 @@ def tile_list_guided_latent_decode_kernel(
             for g in range(groups)
         ]
 
-        def round_wd(g, u0, u1, w16, copy):
+        def round_wd(g, u0, u1, w16, copy, m0=0, m1=P):
             copy(
-                w16.rearrange("p (u e m j) -> p u m j e", e=2, m=P, j=PACK),
-                wd_raw[g].rearrange("p j (m u e) -> p u m j e", u=2, e=2)[:, u0:u1],
+                w16.rearrange("p (u e m j) -> p u m j e", e=2, m=P, j=PACK)[:, :, m0:m1],
+                wd_raw[g].rearrange("p j (m u e) -> p u m j e", u=2, e=2)[:, u0:u1, m0:m1],
             )
 
         def quantize_wd(g, u0, u1, w16, copy):
@@ -259,7 +261,9 @@ def tile_list_guided_latent_decode_kernel(
         def project_half(h, g, free, y):
             for t in range(PACK):
                 project(h, g, t, free[t], y)
-                if t % 2:
+                if (h, g) == (0, 0) and t < 2:
+                    nc.scalar.dma_start(rows(g)[:, t, :HALF], y[:, t, :])
+                elif t % 2:
                     nc.scalar.dma_start(rows(g)[:, t - 1 : t + 1, h * HALF : (h + 1) * HALF], y[:, t - 1 : t + 1, :])
             return y
 
@@ -317,7 +321,10 @@ def tile_list_guided_latent_decode_kernel(
         quantize_wd(0, 0, 2, g_flat[:, PACK * S - HALF :].bitcast(BF16), on_s)
         quantize_z(0)
         gather_g(PACK - 1, HALF, S)
-        quantize_wd(1, 0, 2, half16("wd16", "wc16_0")[:], on_s)
+        wd16 = half16("wd16", "wc16_0")
+        round_wd(1, 0, 2, wd16[:], on_s, 0, SHARE)
+        round_wd(1, 0, 2, wd16[:], on_v, SHARE, P)
+        quantize(wd_q[1][0][:], wd_q[1][1][:], wd16[:])
         for r in range(per_half):
             add_latents(per_half + r)
 
@@ -337,7 +344,8 @@ def tile_list_guided_latent_decode_kernel(
         order = [(0, 0), (0, 1), (1, 0), (1, 1), (0, 2), (1, 2)]
         for i, (h, g) in enumerate(order):
             y16 = half16("y16", "h16")[:]
-            weave(units[i][:, :, :SPLIT], y16[:, : PACK * SPLIT], on_v)
-            weave(units[i][:, :, SPLIT:], y16[:, PACK * SPLIT :], on_s if i + 1 == len(order) else on_v)
+            cut = LAST if i + 1 == len(order) else SPLIT
+            weave(units[i][:, :, :cut], y16[:, : PACK * cut], on_v)
+            weave(units[i][:, :, cut:], y16[:, PACK * cut :], on_s if i + 1 == len(order) else on_v)
             planes(g, h, y16)
         store_scales(0, groups, [nc.scalar, nc.sync])

@@ -25,7 +25,7 @@ HALF = 512
 QUADS = 4
 SPLIT = 256
 LAST = 256
-SHARE = 96
+SHARE = 72
 
 
 def tile_list_guided_latent_decode_kernel(
@@ -46,63 +46,53 @@ def tile_list_guided_latent_decode_kernel(
         offsets = keep.tile([P, S // 16], U16, name="offsets")
         nc.sync.dma_start(offsets[:], offs)
 
-        tab_s = keep.tile([P, passes * T // 4], I32, name="tab_s", align_bytes=64)
-        nc.gpsimd.memset(tab_s[:, : T // 4], 0)
-        nc.vector.memset(tab_s[:, T // 4 :], 0)
+        def slot(name, tag, shape, dtype):
+            return keep.tile(shape, dtype, name=name, tag=tag, align_bytes=64)
+
+        tab_s = slot("tab_s", "slot_a", [P, T // 4], I32)
+        nc.gpsimd.memset(tab_s[:], 0)
         wu_s = keep.tile([P, passes * H // 4], I32, name="wu_s", align_bytes=64)
         nc.vector.memset(wu_s[:], 0)
+        moved = keep.tile([P, S // 4], I32, name="moved", align_bytes=64)
+        nc.vector.memset(moved[:], 0)
         ident = keep.tile([P, P], F32, name="ident")
         make_identity(nc, ident[:])
 
-        def load_table(a):
-            t = keep.tile([P, T], I32, name="tab_w%d" % a, tag="tab_w%d" % a, align_bytes=64)
+        def load_table(a, tag):
+            t = slot("tab_w", tag, [P, T], I32)
             nc.sync.dma_start(t[:], tab_words[a].rearrange("p t i -> p (t i)").bitcast(I32))
-            return t
+            tab_w[a] = t
 
-        def load_wc(a):
-            t = keep.tile([P, PACK, H], F32, name="wc_raw%d" % a, tag="wc_raw%d" % a, align_bytes=64)
+        def load_wc(a, tag):
+            t = slot("wc_raw", tag, [P, PACK, H], F32)
             nc.sync.dma_start(t[:], wc[a * KP : (a + 1) * KP, :].rearrange("(p j) c -> p j c", j=PACK))
-            return t
+            wc_raw[a] = t
 
-        def load_g(t):
-            x = keep.tile([P, T], F32, name="g_tab%d" % t)
+        def load_g(t, tag):
+            x = slot("g_tab", tag, [P, T], F32)
             nc.sync.dma_start(x[:], gT.rearrange("(p t) c -> p t c", t=PACK)[:, t, :])
-            return x
+            g_tab[t] = x
 
-        def load_wd(g0, g1):
-            if g0 == 1:
-                x = keep.tile([P, PACK, KP], F32, name="wd_raw", tag="wd_raw1")
-            else:
-                x = ring.tile([P, PACK, KP], F32, name="wd_raw", tag="big", bufs=4)
-            nc.sync.dma_start(x[:], wd[:, g0 * KP : g1 * KP].rearrange("(p j) c -> p j c", j=PACK))
-            for g in range(g0, g1):
-                wd_raw[g] = x[:, :, (g - g0) * KP : (g - g0 + 1) * KP]
+        def load_wd(g, tag):
+            x = slot("wd_raw", tag, [P, PACK, KP], F32)
+            nc.sync.dma_start(x[:], wd[:, g * KP : (g + 1) * KP].rearrange("(p j) c -> p j c", j=PACK))
+            wd_raw[g] = x[:]
 
         ts32 = tab_scales.bitcast(I32)
         us32 = wu_scales.bitcast(I32)
-        wu_w = [keep.tile([P, 2 * H // 4], I32, name="wu_w%d" % a, align_bytes=64) for a in range(passes)]
-
-        def load_planes(tile, rows):
-            by_row = rows.rearrange("a (q r) n -> r q a n", r=4)
-            for r in range(4):
-                nc.sync.dma_start(tile[r:P:32, :].rearrange("q (a n) -> q a n", a=passes), by_row[r])
+        wu_w = keep.tile([P, passes, 2 * H // 4], I32, name="wu_w", align_bytes=64)
 
         tab_w, wc_raw, g_tab, wd_raw = {}, {}, {}, {}
-        load_planes(tab_s, ts32)
-        nc.sync.dma_start(wu_w[0][:], wu_words[0].bitcast(I32))
-        tab_w[0] = load_table(0)
-        wc_raw[0] = load_wc(0)
-        wc_raw[1] = load_wc(1)
-        tab_w[1] = load_table(1)
-        load_planes(wu_s, us32)
-        nc.sync.dma_start(wu_w[1][:], wu_words[1].bitcast(I32))
-        g_tab[0] = load_g(0)
-        g_tab[1] = load_g(1)
-        g_tab[2] = load_g(2)
-        g_tab[3] = load_g(3)
-        load_wd(0, 1)
-        load_wd(1, 2)
-        load_wd(2, 3)
+        by_row = ts32.rearrange("a (q r) n -> r q a n", r=4)
+        for r in range(4):
+            nc.sync.dma_start(tab_s[r:P:16, :], by_row[r])
+        nc.sync.dma_start(wu_w[:], wu_words.bitcast(I32).rearrange("a p n -> p a n"))
+        load_table(0, "slot_b")
+        load_table(1, "slot_c")
+        load_wc(0, "slot_d")
+        by_row = us32.rearrange("a (q r) n -> r q a n", r=4)
+        for r in range(4):
+            nc.sync.dma_start(wu_s[r:P:32, :].rearrange("q (a n) -> q a n", a=passes), by_row[r])
 
         v_w, v_s, wc_q = {}, {}, {}
 
@@ -114,33 +104,44 @@ def tile_list_guided_latent_decode_kernel(
             for h in range(h0, h1):
                 v_w[a, h] = x[:, (h - h0) * HALF : (h - h0 + 1) * HALF]
 
-        def gather_scales(a, h0, h1, tag):
-            x = keep.tile([P, (h1 - h0) * HALF], U8, name="v_s", tag=tag, align_bytes=64)
-            nc.vector.tensor_copy(
-                x[:],
-                tab_s[:].bitcast(U8)[:, a * T : (a + 1) * T].indirect(offsets[:, h0 * HALF // 16 : h1 * HALF // 16]),
-            )
-            for h in range(h0, h1):
-                v_s[a, h] = x[:, (h - h0) * HALF : (h - h0 + 1) * HALF]
+        picked = keep.tile([P, S], U8, name="picked", align_bytes=64)
+        nc.vector.tensor_copy(picked[:], tab_s[:].bitcast(U8).indirect(offsets[:]))
+        nc.sync.dma_start(moved[: P - 16, :], picked[16:, :].bitcast(I32))
+        for h in range(halves):
+            v_s[0, h] = picked[:, h * HALF : (h + 1) * HALF]
+            v_s[1, h] = moved[:].bitcast(U8)[:, h * HALF : (h + 1) * HALF]
 
-        def quantize_wc(a):
+        def quantize(codes, scales, x16):
+            width = codes.shape[1] // 2
+            for c0 in (0, width):
+                nc.vector.quantize_mx(
+                    out=codes[:, c0 : c0 + width].bitcast(FP8X4),
+                    scales=scales[:, c0 : c0 + width],
+                    in_=x16[:, PACK * c0 : PACK * (c0 + width)],
+                )
+
+        on_s, on_v = nc.scalar.copy, nc.vector.tensor_copy
+
+        def quantize_wc(a, second):
             w16 = keep.tile([P, H * PACK], BF16, name="wc16", tag="wc16_%d" % a, align_bytes=64)
-            nc.scalar.copy(
-                w16[:].rearrange("p (c i j) -> p c j i", i=2, j=PACK),
-                wc_raw[a][:].rearrange("p j (c i) -> p c j i", i=2),
-            )
+            for c0, copy in ((0, on_v), (H // 4, second)):
+                copy(
+                    w16[:].rearrange("p (c i j) -> p c j i", i=2, j=PACK)[:, c0 : c0 + H // 4],
+                    wc_raw[a][:].rearrange("p j (c i) -> p c j i", i=2)[:, c0 : c0 + H // 4],
+                )
             codes = keep.tile([P, H], U32, name="wc_c%d" % a, align_bytes=64)
             scales = keep.tile([P, H], U8, name="wc_s%d" % a, align_bytes=64)
-            nc.vector.quantize_mx(out=codes[:].bitcast(FP8X4), scales=scales[:], in_=w16[:])
+            quantize(codes[:], scales[:], w16[:])
             wc_q[a] = (codes, scales)
 
-        gather_scales(0, 0, 2, "v_s0")
+        load_g(0, "slot_a")
         gather_words(0, 0, 2, "v_w0")
-        gather_scales(1, 0, 2, "tab_w0")
-        quantize_wc(0)
+        load_wc(1, "slot_b")
         gather_words(1, 0, 1, "v_w1")
-        quantize_wc(1)
-        gather_words(1, 1, 2, "wc_raw1")
+        gather_words(1, 1, 2, "v_w2")
+        load_g(1, "slot_c")
+        quantize_wc(0, on_s)
+        load_g(2, "slot_d")
 
         g_flat = keep.tile([P, PACK * S + HALF], F32, name="g_flat", align_bytes=64)
         g_pick = g_flat[:, : PACK * S].rearrange("p (t s) -> p t s", t=PACK)
@@ -160,7 +161,7 @@ def tile_list_guided_latent_decode_kernel(
             cols = slice(r * P, (r + 1) * P)
             for i, a in enumerate(range(passes)):
                 if which == "b":
-                    rhs, rhs_scale = wu_w[a][:].bitcast(FP4X4), wu_s_bytes[:, a * H : (a + 1) * H]
+                    rhs, rhs_scale = wu_w[:, a, :].bitcast(FP4X4), wu_s_bytes[:, a * H : (a + 1) * H]
                 else:
                     rhs, rhs_scale = wc_q[a][0][:].bitcast(FP8X4), wc_q[a][1][:]
                 nc.tensor.matmul_mx(
@@ -194,10 +195,13 @@ def tile_list_guided_latent_decode_kernel(
 
         def add_latents(b):
             h, r = divmod(b, per_half)
-            if r == 0:
-                z16[h] = keep.tile([P, HALF * PACK], BF16, name="z16", tag=["wc16_1", "wc16_0"][h], align_bytes=64)
+            if b == 0:
+                whole = half16("z16", "wc16_1")
+                z16[0], z16[1] = whole[:, : 2 * KP], whole[:, 2 * KP :]
+            elif h == 1 and r % 2 == 0:
+                z16[b // 2] = half16("z16", "h16")[:, : 2 * KP]
             nc.vector.tensor_tensor(
-                z16[h][:, r * KP : (r + 1) * KP].rearrange("p (c i t) -> p c t i", i=2, t=PACK),
+                z16[b // 2][:, r % 2 * KP : (r % 2 + 1) * KP].rearrange("p (c i t) -> p c t i", i=2, t=PACK),
                 turned[b].rearrange("p t (c i) -> p c t i", i=2),
                 g_pick[:, :, b * P : (b + 1) * P].rearrange("p t (c i) -> p c t i", i=2),
                 ADD,
@@ -206,18 +210,11 @@ def tile_list_guided_latent_decode_kernel(
         z_c = {}
         z_s = [keep.tile([P, HALF], U8, name="z_s%d" % h, align_bytes=64) for h in range(halves)]
 
-        def quantize(codes, scales, x16):
-            width = codes.shape[1] // 2
-            for c0 in (0, width):
-                nc.vector.quantize_mx(
-                    out=codes[:, c0 : c0 + width].bitcast(FP8X4),
-                    scales=scales[:, c0 : c0 + width],
-                    in_=x16[:, PACK * c0 : PACK * (c0 + width)],
-                )
-
         def quantize_z(h):
             z_c[h] = keep.tile([P, HALF], U32, name="z_c", tag="z_c%d" % h, align_bytes=64)
-            quantize(z_c[h][:], z_s[h][:], z16[h][:])
+            for i in range(2):
+                cols = slice(i * HALF // 2, (i + 1) * HALF // 2)
+                nc.vector.quantize_mx(out=z_c[h][:, cols].bitcast(FP8X4), scales=z_s[h][:, cols], in_=z16[2 * h + i])
 
         wd_q = [
             (
@@ -238,7 +235,9 @@ def tile_list_guided_latent_decode_kernel(
             cols = slice(2 * P * u0, 2 * P * u1)
             nc.vector.quantize_mx(out=wd_q[g][0][:, cols].bitcast(FP8X4), scales=wd_q[g][1][:, cols], in_=w16)
 
-        y_s = keep.tile([P, groups * S], U8, name="y_s", align_bytes=64)
+        y_early = keep.tile([P, (groups - 1) * S], U8, name="y_early", align_bytes=64)
+        y_last = keep.tile([P, S], U8, name="y_last", align_bytes=64)
+        y_s = [y_early[:, :S], y_early[:, S:], y_last[:]]
         words32 = out_1.rearrange("g p m t -> g p (m t)").bitcast(I32)
         scales32 = out_2.bitcast(I32)
 
@@ -258,8 +257,8 @@ def tile_list_guided_latent_decode_kernel(
         def rows(g):
             return out_0[g * KP : (g + 1) * KP, :].rearrange("(p t) s -> p t s", t=PACK)
 
-        def project_half(h, g, free, y):
-            for t in range(PACK):
+        def project_half(h, g, free, y, t0=0, t1=PACK):
+            for t in range(t0, t1):
                 project(h, g, t, free[t], y)
                 if (h, g) == (0, 0) and t < 2:
                     nc.scalar.dma_start(rows(g)[:, t, :HALF], y[:, t, :])
@@ -272,7 +271,7 @@ def tile_list_guided_latent_decode_kernel(
             for u in range(2):
                 for h in range(halves):
                     for e in range(2):
-                        project(h, g, 2 * u + e, banks[4 * (1 - u) + 2 * h + e], parts[h])
+                        project(h, g, 2 * u + e, banks[2 * h + e], parts[h])
                 nc.scalar.dma_start(rows(g)[:, 2 * u : 2 * u + 2, :], y[:, 2 * u : 2 * u + 2, :])
             return parts
 
@@ -285,42 +284,58 @@ def tile_list_guided_latent_decode_kernel(
 
         y_c = [keep.tile([P, S], U32, name="y_c%d" % g, align_bytes=64) for g in range(groups)]
 
-        def planes(g, h, y16):
-            c0 = h * HALF
-            quantize(y_c[g][:, c0 : c0 + HALF], y_s[:, g * S + c0 : g * S + c0 + HALF], y16)
-            if g == groups - 1:
-                nc.sync.dma_start(words32[g][:, c0 : c0 + HALF], y_c[g][:, c0 : c0 + HALF].bitcast(I32))
-            elif h == halves - 1:
-                nc.sync.dma_start(words32[g], y_c[g][:].bitcast(I32))
-
-        def store_scales(g0, g1, queues):
+        def store_scales(g0, g1, tile, queues):
             by_row = scales32[g0:g1].rearrange("g (q r) n -> r q g n", r=4)
             for r in range(4):
                 queues[r % len(queues)].dma_start(
-                    by_row[r], y_s[r:P:32, :].bitcast(I32).rearrange("q (g n) -> q g n", g=g1 - g0)
+                    by_row[r], tile[r:P:32, :].bitcast(I32).rearrange("q (g n) -> q g n", g=g1 - g0)
                 )
+
+        def planes(h, g, y16):
+            cols = slice(h * HALF, (h + 1) * HALF)
+            if (h, g) == (halves - 1, groups - 1):
+                quantize(y_c[g][:, cols], y_s[g][:, cols], y16)
+            else:
+                nc.vector.quantize_mx(out=y_c[g][:, cols].bitcast(FP8X4), scales=y_s[g][:, cols], in_=y16)
+            if g == groups - 1:
+                nc.sync.dma_start(words32[g][:, cols], y_c[g][:, cols].bitcast(I32))
+            elif h == halves - 1:
+                nc.sync.dma_start(words32[g], y_c[g][:].bitcast(I32))
+            if (h, g) == (halves - 1, groups - 2):
+                store_scales(0, groups - 1, y_early, [nc.sync])
 
         def half16(name, tag):
             if tag == "h16":
-                return ring.tile([P, HALF * PACK], BF16, name=name, tag=tag, align_bytes=64, bufs=3)
+                return ring.tile([P, HALF * PACK], BF16, name=name, tag=tag, align_bytes=64, bufs=2)
             return keep.tile([P, HALF * PACK], BF16, name=name, tag=tag, align_bytes=64)
 
-        on_s, on_v = nc.scalar.copy, nc.vector.tensor_copy
         low, high = banks[:4], banks[4:]
+        gather_g(0, 0, S)
+        load_g(3, "slot_a")
+        quantize_wc(1, on_v)
+        load_wd(0, "slot_b")
         for b in range(blocks):
-            predict(b, "a", banks[2 * b % 8])
-            predict(b, "b", banks[(2 * b + 1) % 8])
+            predict(b, "b", banks[b])
+        for b in range(blocks):
+            predict(b, "a", banks[b])
         for b in range(blocks):
             turn(b, banks[b])
-        for t in range(PACK - 1):
-            gather_g(t, 0, S)
+        gather_g(1, 0, S)
+        load_wd(1, "slot_c")
+        gather_g(2, 0, S)
+        load_wd(2, "slot_d")
         gather_g(PACK - 1, 0, HALF // 2)
         gather_g(PACK - 1, HALF // 2, HALF)
         for r in range(per_half):
             add_latents(r)
-        quantize_wd(0, 0, 2, g_flat[:, PACK * S - HALF :].bitcast(BF16), on_s)
+        wd16 = g_flat[:, PACK * S - HALF :].bitcast(BF16)
+        quantize_wd(0, 0, 1, wd16[:, 2 * KP :], on_s)
         quantize_z(0)
-        gather_g(PACK - 1, HALF, S)
+        quantize_wd(0, 1, 2, wd16[:, : 2 * KP], on_s)
+        y00 = slot("y00", "slot_b", [P, PACK, HALF], F32)
+        project_half(0, 0, low, y00[:], 0, 2)
+        gather_g(PACK - 1, HALF, S - HALF // 2)
+        gather_g(PACK - 1, S - HALF // 2, S)
         wd16 = half16("wd16", "wc16_0")
         round_wd(1, 0, 2, wd16[:], on_s, 0, SHARE)
         round_wd(1, 0, 2, wd16[:], on_v, SHARE, P)
@@ -329,23 +344,29 @@ def tile_list_guided_latent_decode_kernel(
             add_latents(per_half + r)
 
         def y_tile():
-            return ring.tile([P, PACK, HALF], F32, name="y", tag="big", bufs=4)[:]
+            return ring.tile([P, PACK, HALF], F32, name="y", tag="big", bufs=3)[:]
 
-        y00 = keep.tile([P, PACK, HALF], F32, name="y00", tag="wd_raw1")
-        units = [project_half(0, 0, low, y00[:]), project_half(0, 1, low, y_tile())]
+        units = [project_half(0, 0, low, y00[:], 2, PACK), project_half(0, 1, low, y_tile())]
         quantize_z(1)
-        units.append(project_half(1, 0, high, y_tile()))
+        units.append(project_half(1, 0, low, y_tile()))
+        y16 = {(0, 0): weave(units[0], half16("y16", "h16")[:], on_v)}
         wd16 = half16("wd16", "h16")
         for u in range(2):
             round_wd(2, u, u + 1, wd16[:, 2 * KP * u : 2 * KP * (u + 1)], on_v)
-        quantize(wd_q[2][0][:], wd_q[2][1][:], wd16[:])
+        planes(0, 0, y16[0, 0])
+        nc.vector.quantize_mx(out=wd_q[2][0][:].bitcast(FP8X4), scales=wd_q[2][1][:], in_=wd16[:])
         units.append(project_half(1, 1, low, y_tile()))
         units.extend(project_group(2, g_pick))
-        order = [(0, 0), (0, 1), (1, 0), (1, 1), (0, 2), (1, 2)]
-        for i, (h, g) in enumerate(order):
-            y16 = half16("y16", "h16")[:]
-            cut = LAST if i + 1 == len(order) else SPLIT
-            weave(units[i][:, :, :cut], y16[:, : PACK * cut], on_v)
-            weave(units[i][:, :, cut:], y16[:, PACK * cut :], on_s if i + 1 == len(order) else on_v)
-            planes(g, h, y16)
-        store_scales(0, groups, [nc.scalar, nc.sync])
+        y16[1, 0] = weave(units[2], half16("y16", "h16")[:], on_v)
+        y16[0, 1] = weave(units[1], half16("y16", "h16")[:], on_v)
+        planes(1, 0, y16[1, 0])
+        y16[1, 1] = weave(units[3], half16("y16", "h16")[:], on_v)
+        planes(0, 1, y16[0, 1])
+        planes(1, 1, y16[1, 1])
+        y16[0, 2] = weave(units[4], half16("y16", "h16")[:], on_v)
+        last = half16("y16", "wc16_0")[:]
+        weave(units[5][:, :, :LAST], last[:, : PACK * LAST], on_v)
+        weave(units[5][:, :, LAST:], last[:, PACK * LAST :], on_s)
+        planes(0, 2, y16[0, 2])
+        planes(1, 2, last)
+        store_scales(groups - 1, groups, y_last, [nc.scalar, nc.sync])

@@ -43,6 +43,8 @@ def tile_list_guided_latent_decode_kernel(
         ring = ctx.enter_context(tc.tile_pool(name="ring", bufs=2))
         psum = ctx.enter_context(tc.psum_pool(name="psum", bufs=1))
 
+        wu_w = keep.tile([P, passes, 2 * H // 4], I32, name="wu_w", align_bytes=64)
+        nc.sync.dma_start(wu_w[:], wu_words.bitcast(I32).rearrange("a p n -> p a n"))
         offsets = keep.tile([P, S // 16], U16, name="offsets")
         nc.sync.dma_start(offsets[:], offs)
 
@@ -80,13 +82,11 @@ def tile_list_guided_latent_decode_kernel(
 
         ts32 = tab_scales.bitcast(I32)
         us32 = wu_scales.bitcast(I32)
-        wu_w = keep.tile([P, passes, 2 * H // 4], I32, name="wu_w", align_bytes=64)
 
         tab_w, wc_raw, g_tab, wd_raw = {}, {}, {}, {}
         by_row = ts32.rearrange("a (q r) n -> r q a n", r=4)
         for r in range(4):
             nc.sync.dma_start(tab_s[r:P:16, :], by_row[r])
-        nc.sync.dma_start(wu_w[:], wu_words.bitcast(I32).rearrange("a p n -> p a n"))
         load_table(0, "slot_b")
         load_table(1, "slot_c")
         load_wc(0, "slot_d")
@@ -237,7 +237,7 @@ def tile_list_guided_latent_decode_kernel(
 
         y_early = keep.tile([P, (groups - 1) * S], U8, name="y_early", align_bytes=64)
         y_last = keep.tile([P, S], U8, name="y_last", align_bytes=64)
-        y_s = [y_early[:, :S], y_early[:, S:], y_last[:]]
+        y_s = [y_early[4:, :S], y_early[4:, S:], y_last[8:, :]]
         words32 = out_1.rearrange("g p m t -> g p (m t)").bitcast(I32)
         scales32 = out_2.bitcast(I32)
 
@@ -284,11 +284,11 @@ def tile_list_guided_latent_decode_kernel(
 
         y_c = [keep.tile([P, S], U32, name="y_c%d" % g, align_bytes=64) for g in range(groups)]
 
-        def store_scales(g0, g1, tile, queues):
+        def store_scales(g0, g1, tile, first, queues):
             by_row = scales32[g0:g1].rearrange("g (q r) n -> r q g n", r=4)
             for r in range(4):
                 queues[r % len(queues)].dma_start(
-                    by_row[r], tile[r:P:32, :].bitcast(I32).rearrange("q (g n) -> q g n", g=g1 - g0)
+                    by_row[r], tile[first + r : P : 32, :].bitcast(I32).rearrange("q (g n) -> q g n", g=g1 - g0)
                 )
 
         def planes(h, g, y16):
@@ -302,7 +302,7 @@ def tile_list_guided_latent_decode_kernel(
             elif h == halves - 1:
                 nc.sync.dma_start(words32[g], y_c[g][:].bitcast(I32))
             if (h, g) == (halves - 1, groups - 2):
-                store_scales(0, groups - 1, y_early, [nc.sync])
+                store_scales(0, groups - 1, y_early, 4, [nc.sync])
 
         def half16(name, tag):
             if tag == "h16":
@@ -369,4 +369,4 @@ def tile_list_guided_latent_decode_kernel(
         weave(units[5][:, :, LAST:], last[:, PACK * LAST :], on_s)
         planes(0, 2, y16[0, 2])
         planes(1, 2, last)
-        store_scales(groups - 1, groups, y_last, [nc.scalar, nc.sync])
+        store_scales(groups - 1, groups, y_last, 8, [nc.scalar, nc.sync])

@@ -261,19 +261,16 @@ def tile_list_guided_latent_decode_kernel(
             for t in range(t0, t1):
                 project(h, g, t, free[t], y)
                 if (h, g) == (0, 0) and t < 2:
-                    nc.scalar.dma_start(rows(g)[:, t, :HALF], y[:, t, :])
+                    nc.sync.dma_start(rows(g)[:, t, :HALF], y[:, t, :])
                 elif t % 2:
-                    nc.scalar.dma_start(rows(g)[:, t - 1 : t + 1, h * HALF : (h + 1) * HALF], y[:, t - 1 : t + 1, :])
+                    nc.sync.dma_start(rows(g)[:, t - 1 : t + 1, h * HALF : (h + 1) * HALF], y[:, t - 1 : t + 1, :])
             return y
 
-        def project_group(g, y):
-            parts = [y[:, :, h * HALF : (h + 1) * HALF] for h in range(halves)]
-            for u in range(2):
-                for h in range(halves):
-                    for e in range(2):
-                        project(h, g, 2 * u + e, banks[2 * h + e], parts[h])
-                nc.scalar.dma_start(rows(g)[:, 2 * u : 2 * u + 2, :], y[:, 2 * u : 2 * u + 2, :])
-            return parts
+        def project_pair(g, u, y):
+            for h in range(halves):
+                for e in range(2):
+                    project(h, g, 2 * u + e, banks[2 * h + e], y[:, :, h * HALF : (h + 1) * HALF])
+            nc.scalar.dma_start(rows(g)[:, 2 * u : 2 * u + 2, :], y[:, 2 * u : 2 * u + 2, :])
 
         def weave(y, y16, copy):
             copy(
@@ -299,10 +296,6 @@ def tile_list_guided_latent_decode_kernel(
                 nc.vector.quantize_mx(out=y_c[g][:, cols].bitcast(FP8X4), scales=y_s[g][:, cols], in_=y16)
             if g == groups - 1:
                 nc.sync.dma_start(words32[g][:, cols], y_c[g][:, cols].bitcast(I32))
-            elif h == halves - 1:
-                nc.sync.dma_start(words32[g], y_c[g][:].bitcast(I32))
-            if (h, g) == (halves - 1, groups - 2):
-                store_scales(0, groups - 1, y_early, 4, [nc.sync])
 
         def half16(name, tag):
             if tag == "h16":
@@ -356,13 +349,18 @@ def tile_list_guided_latent_decode_kernel(
         planes(0, 0, y16[0, 0])
         nc.vector.quantize_mx(out=wd_q[2][0][:].bitcast(FP8X4), scales=wd_q[2][1][:], in_=wd16[:])
         units.append(project_half(1, 1, low, y_tile()))
-        units.extend(project_group(2, g_pick))
-        y16[1, 0] = weave(units[2], half16("y16", "h16")[:], on_v)
+        project_pair(2, 0, g_pick)
+        project_pair(2, 1, g_pick)
+        units.extend(g_pick[:, :, h * HALF : (h + 1) * HALF] for h in range(halves))
         y16[0, 1] = weave(units[1], half16("y16", "h16")[:], on_v)
-        planes(1, 0, y16[1, 0])
-        y16[1, 1] = weave(units[3], half16("y16", "h16")[:], on_v)
+        y16[1, 0] = weave(units[2], half16("y16", "h16")[:], on_v)
         planes(0, 1, y16[0, 1])
+        y16[1, 1] = weave(units[3], half16("y16", "h16")[:], on_v)
+        planes(1, 0, y16[1, 0])
+        nc.sync.dma_start(words32[0], y_c[0][:].bitcast(I32))
         planes(1, 1, y16[1, 1])
+        nc.sync.dma_start(words32[1], y_c[1][:].bitcast(I32))
+        store_scales(0, groups - 1, y_early, 4, [nc.sync])
         y16[0, 2] = weave(units[4], half16("y16", "h16")[:], on_v)
         last = half16("y16", "wc16_0")[:]
         weave(units[5][:, :, :LAST], last[:, : PACK * LAST], on_v)

@@ -352,12 +352,12 @@ def tile_list_guided_latent_decode_kernel(
         project_pair(2, 0, g_pick)
         project_pair(2, 1, g_pick)
         units.extend(g_pick[:, :, h * HALF : (h + 1) * HALF] for h in range(halves))
-        y16[0, 1] = weave(units[1], half16("y16", "h16")[:], on_v)
         y16[1, 0] = weave(units[2], half16("y16", "h16")[:], on_v)
-        planes(0, 1, y16[0, 1])
-        y16[1, 1] = weave(units[3], half16("y16", "h16")[:], on_v)
+        y16[0, 1] = weave(units[1], half16("y16", "h16")[:], on_v)
         planes(1, 0, y16[1, 0])
         nc.sync.dma_start(words32[0], y_c[0][:].bitcast(I32))
+        y16[1, 1] = weave(units[3], half16("y16", "h16")[:], on_v)
+        planes(0, 1, y16[0, 1])
         planes(1, 1, y16[1, 1])
         nc.sync.dma_start(words32[1], y_c[1][:].bitcast(I32))
         store_scales(0, groups - 1, y_early, 4, [nc.sync])

from contextlib import ExitStack

import concourse.mybir as mybir
from concourse.masks import make_identity

K, T, S, H, N = 1024, 2048, 1024, 512, 1536
FLOPS = 2 * (2 * K * H * S) + 2 * H * N * S

F32 = mybir.dt.float32
BF16 = mybir.dt.bfloat16
I32 = mybir.dt.int32
U32 = mybir.dt.uint32
U16 = mybir.dt.uint16
U8 = mybir.dt.uint8
FP8X4 = mybir.dt.float8_e4m3fn_x4
FP4X4 = mybir.dt.float4_e2m1fn_x4
COPY = mybir.ActivationFunctionType.Copy
ADD = mybir.AluOpType.add

P = 128
PACK = 4
KP = P * PACK
BANK = 512
HALF = 512
QUADS = 4
SPLIT = 256
LAST = 256
SHARE = 72


def tile_list_guided_latent_decode_kernel(
    tc, tab_words, tab_scales, offs, wc, wu_words, wu_scales, gT, wd, out_0, out_1, out_2
):
    nc = tc.nc
    passes = K // KP
    groups = N // KP
    halves = S // HALF
    blocks = S // P
    per_half = HALF // P

    with ExitStack() as ctx:
        keep = ctx.enter_context(tc.tile_pool(name="keep", bufs=1))
        ring = ctx.enter_context(tc.tile_pool(name="ring", bufs=2))
        psum = ctx.enter_context(tc.psum_pool(name="psum", bufs=1))

        wu_w = keep.tile([P, passes, 2 * H // 4], I32, name="wu_w", align_bytes=64)
        nc.sync.dma_start(wu_w[:], wu_words.bitcast(I32).rearrange("a p n -> p a n"))
        offsets = keep.tile([P, S // 16], U16, name="offsets")
        nc.sync.dma_start(offsets[:], offs)

        def slot(name, tag, shape, dtype):
            return keep.tile(shape, dtype, name=name, tag=tag, align_bytes=64)

        tab_s = slot("tab_s", "slot_a", [P, T // 4], I32)
        nc.gpsimd.memset(tab_s[:], 0)
        wu_s = keep.tile([P, passes * H // 4], I32, name="wu_s", align_bytes=64)
        nc.vector.memset(wu_s[:], 0)
        moved = keep.tile([P, S // 4], I32, name="moved", align_bytes=64)
        nc.vector.memset(moved[:], 0)
        ident = keep.tile([P, P], F32, name="ident")
        make_identity(nc, ident[:])

        def load_table(a, tag):
            t = slot("tab_w", tag, [P, T], I32)
            nc.sync.dma_start(t[:], tab_words[a].rearrange("p t i -> p (t i)").bitcast(I32))
            tab_w[a] = t

        def load_wc(a, tag):
            t = slot("wc_raw", tag, [P, PACK, H], F32)
            nc.sync.dma_start(t[:], wc[a * KP : (a + 1) * KP, :].rearrange("(p j) c -> p j c", j=PACK))
            wc_raw[a] = t

        def load_g(t, tag):
            x = slot("g_tab", tag, [P, T], F32)
            nc.sync.dma_start(x[:], gT.rearrange("(p t) c -> p t c", t=PACK)[:, t, :])
            g_tab[t] = x

        def load_wd(g, tag):
            x = slot("wd_raw", tag, [P, PACK, KP], F32)
            nc.sync.dma_start(x[:], wd[:, g * KP : (g + 1) * KP].rearrange("(p j) c -> p j c", j=PACK))
            wd_raw[g] = x[:]

        ts32 = tab_scales.bitcast(I32)
        us32 = wu_scales.bitcast(I32)

        tab_w, wc_raw, g_tab, wd_raw = {}, {}, {}, {}
        by_row = ts32.rearrange("a (q r) n -> r q a n", r=4)
        for r in range(4):
            nc.sync.dma_start(tab_s[r:P:16, :], by_row[r])
        load_table(0, "slot_b")
        load_table(1, "slot_c")
        load_wc(0, "slot_d")
        by_row = us32.rearrange("a (q r) n -> r q a n", r=4)
        for r in range(4):
            nc.sync.dma_start(wu_s[r:P:32, :].rearrange("q (a n) -> q a n", a=passes), by_row[r])

        v_w, v_s, wc_q = {}, {}, {}

        def gather_words(a, h0, h1, tag):
            x = keep.tile([P, (h1 - h0) * HALF], U32, name="v_w", tag=tag, align_bytes=64)
            nc.vector.tensor_copy(
                x[:], tab_w[a][:].bitcast(U32).indirect(offsets[:, h0 * HALF // 16 : h1 * HALF // 16])
            )
            for h in range(h0, h1):
                v_w[a, h] = x[:, (h - h0) * HALF : (h - h0 + 1) * HALF]

        picked = keep.tile([P, S], U8, name="picked", align_bytes=64)
        nc.vector.tensor_copy(picked[:], tab_s[:].bitcast(U8).indirect(offsets[:]))
        nc.sync.dma_start(moved[: P - 16, :], picked[16:, :].bitcast(I32))
        for h in range(halves):
            v_s[0, h] = picked[:, h * HALF : (h + 1) * HALF]
            v_s[1, h] = moved[:].bitcast(U8)[:, h * HALF : (h + 1) * HALF]

        def quantize(codes, scales, x16):
            width = codes.shape[1] // 2
            for c0 in (0, width):
                nc.vector.quantize_mx(
                    out=codes[:, c0 : c0 + width].bitcast(FP8X4),
                    scales=scales[:, c0 : c0 + width],
                    in_=x16[:, PACK * c0 : PACK * (c0 + width)],
                )

        on_s, on_v = nc.scalar.copy, nc.vector.tensor_copy

        def quantize_wc(a, second):
            w16 = keep.tile([P, H * PACK], BF16, name="wc16", tag="wc16_%d" % a, align_bytes=64)
            for c0, copy in ((0, on_v), (H // 4, second)):
                copy(
                    w16[:].rearrange("p (c i j) -> p c j i", i=2, j=PACK)[:, c0 : c0 + H // 4],
                    wc_raw[a][:].rearrange("p j (c i) -> p c j i", i=2)[:, c0 : c0 + H // 4],
                )
            codes = keep.tile([P, H], U32, name="wc_c%d" % a, align_bytes=64)
            scales = keep.tile([P, H], U8, name="wc_s%d" % a, align_bytes=64)
            quantize(codes[:], scales[:], w16[:])
            wc_q[a] = (codes, scales)

        load_g(0, "slot_a")
        gather_words(0, 0, 2, "v_w0")
        load_wc(1, "slot_b")
        gather_words(1, 0, 1, "v_w1")
        gather_words(1, 1, 2, "v_w2")
        load_g(1, "slot_c")
        quantize_wc(0, on_s)
        load_g(2, "slot_d")

        g_flat = keep.tile([P, PACK * S + HALF], F32, name="g_flat", align_bytes=64)
        g_pick = g_flat[:, : PACK * S].rearrange("p (t s) -> p t s", t=PACK)

        def gather_g(t, c0, c1):
            nc.vector.tensor_copy(
                g_flat[:, t * S + c0 : t * S + c1], g_tab[t][:].indirect(offsets[:, c0 // 16 : c1 // 16])
            )

        wu_s_bytes = wu_s[:].bitcast(U8)
        scaled = {}

        banks = [psum.tile([P, BANK], F32, name="bank%d" % i) for i in range(8)]

        def predict(b, which, bank):
            h, r = divmod(b, per_half)
            cols = slice(r * P, (r + 1) * P)
            for i, a in enumerate(range(passes)):
                if which == "b":
                    rhs, rhs_scale = wu_w[:, a, :].bitcast(FP4X4), wu_s_bytes[:, a * H : (a + 1) * H]
                else:
                    rhs, rhs_scale = wc_q[a][0][:].bitcast(FP8X4), wc_q[a][1][:]
                nc.tensor.matmul_mx(
                    out=bank[:],
                    lhsT=v_w[a, h][:, cols].bitcast(FP8X4),
                    lhsT_scale=v_s[a, h][:, cols],
                    rhs=rhs,
                    rhs_scale=rhs_scale,
                    start=(i == 0),
                    stop=(i == passes - 1),
                )
            x = keep.tile([P, PACK, P], F32, name="s%s%d" % (which, b))
            nc.scalar.activation(
                x[:].rearrange("p (u e) m -> p u m e", e=2),
                bank[:].rearrange("p (m u e) -> p u m e", u=2, e=2),
                COPY,
                scale=0.2 if which == "b" else -0.3,
            )
            scaled.setdefault(b, []).append(x)

        turned = {}

        def turn(b, bank):
            u = bank[:].rearrange("p (t s) -> p t s", t=PACK)
            for t in range(PACK):
                for i, x in enumerate(scaled[b]):
                    nc.tensor.matmul(u[:, t, :], x[:, t, :], ident[:], start=(i == 0), stop=(i == 1), is_transpose=True)
            turned[b] = u

        z16 = {}

        def add_latents(b):
            h, r = divmod(b, per_half)
            if b == 0:
                whole = half16("z16", "wc16_1")
                z16[0], z16[1] = whole[:, : 2 * KP], whole[:, 2 * KP :]
            elif h == 1 and r % 2 == 0:
                z16[b // 2] = half16("z16", "h16")[:, : 2 * KP]
            nc.vector.tensor_tensor(
                z16[b // 2][:, r % 2 * KP : (r % 2 + 1) * KP].rearrange("p (c i t) -> p c t i", i=2, t=PACK),
                turned[b].rearrange("p t (c i) -> p c t i", i=2),
                g_pick[:, :, b * P : (b + 1) * P].rearrange("p t (c i) -> p c t i", i=2),
                ADD,
            )

        z_c = {}
        z_s = [keep.tile([P, HALF], U8, name="z_s%d" % h, align_bytes=64) for h in range(halves)]

        def quantize_z(h):
            z_c[h] = keep.tile([P, HALF], U32, name="z_c", tag="z_c%d" % h, align_bytes=64)
            for i in range(2):
                cols = slice(i * HALF // 2, (i + 1) * HALF // 2)
                nc.vector.quantize_mx(out=z_c[h][:, cols].bitcast(FP8X4), scales=z_s[h][:, cols], in_=z16[2 * h + i])

        wd_q = [
            (
                keep.tile([P, KP], U32, name="wd_c%d" % g, align_bytes=64),
                keep.tile([P, KP], U8, name="wd_s%d" % g, align_bytes=64),
            )
            for g in range(groups)
        ]

        def round_wd(g, u0, u1, w16, copy, m0=0, m1=P):
            copy(
                w16.rearrange("p (u e m j) -> p u m j e", e=2, m=P, j=PACK)[:, :, m0:m1],
                wd_raw[g].rearrange("p j (m u e) -> p u m j e", u=2, e=2)[:, u0:u1, m0:m1],
            )

        def quantize_wd(g, u0, u1, w16, copy):
            round_wd(g, u0, u1, w16, copy)
            cols = slice(2 * P * u0, 2 * P * u1)
            nc.vector.quantize_mx(out=wd_q[g][0][:, cols].bitcast(FP8X4), scales=wd_q[g][1][:, cols], in_=w16)

        y_early = keep.tile([P, (groups - 1) * S], U8, name="y_early", align_bytes=64)
        y_last = keep.tile([P, S], U8, name="y_last", align_bytes=64)
        y_s = [y_early[4:, :S], y_early[4:, S:], y_last[8:, :]]
        words32 = out_1.rearrange("g p m t -> g p (m t)").bitcast(I32)
        scales32 = out_2.bitcast(I32)

        def project(h, g, t, bank, y):
            wcols = slice(t * P, (t + 1) * P)
            nc.tensor.matmul_mx(
                out=bank[:],
                lhsT=wd_q[g][0][:, wcols].bitcast(FP8X4),
                lhsT_scale=wd_q[g][1][:, wcols],
                rhs=z_c[h][:].bitcast(FP8X4),
                rhs_scale=z_s[h][:],
                start=True,
                stop=True,
            )
            nc.scalar.copy(y[:, t, :], bank[:])

        def rows(g):
            return out_0[g * KP : (g + 1) * KP, :].rearrange("(p t) s -> p t s", t=PACK)

        def project_half(h, g, free, y, t0=0, t1=PACK):
            for t in range(t0, t1):
                project(h, g, t, free[t], y)
                if (h, g) == (0, 0) and t < 2:
                    nc.sync.dma_start(rows(g)[:, t, :HALF], y[:, t, :])
                elif t % 2:
                    nc.sync.dma_start(rows(g)[:, t - 1 : t + 1, h * HALF : (h + 1) * HALF], y[:, t - 1 : t + 1, :])
            return y

        def project_pair(g, u, y):
            for h in range(halves):
                for e in range(2):
                    project(h, g, 2 * u + e, banks[2 * h + e], y[:, :, h * HALF : (h + 1) * HALF])
            nc.scalar.dma_start(rows(g)[:, 2 * u : 2 * u + 2, :], y[:, 2 * u : 2 * u + 2, :])

        def weave(y, y16, copy):
            copy(
                y16.rearrange("p (c i t) -> p c t i", i=2, t=PACK),
                y.rearrange("p t (c i) -> p c t i", i=2),
            )
            return y16

        y_c = [keep.tile([P, S], U32, name="y_c%d" % g, align_bytes=64) for g in range(groups)]

        def store_scales(g0, g1, tile, first, queues):
            by_row = scales32[g0:g1].rearrange("g (q r) n -> r q g n", r=4)
            for r in range(4):
                queues[r % len(queues)].dma_start(
                    by_row[r], tile[first + r : P : 32, :].bitcast(I32).rearrange("q (g n) -> q g n", g=g1 - g0)
                )

        def planes(h, g, y16):
            cols = slice(h * HALF, (h + 1) * HALF)
            if (h, g) == (halves - 1, groups - 1):
                quantize(y_c[g][:, cols], y_s[g][:, cols], y16)
            else:
                nc.vector.quantize_mx(out=y_c[g][:, cols].bitcast(FP8X4), scales=y_s[g][:, cols], in_=y16)
            if g == groups - 1:
                nc.sync.dma_start(words32[g][:, cols], y_c[g][:, cols].bitcast(I32))

        def half16(name, tag):
            if tag == "h16":
                return ring.tile([P, HALF * PACK], BF16, name=name, tag=tag, align_bytes=64, bufs=2)
            return keep.tile([P, HALF * PACK], BF16, name=name, tag=tag, align_bytes=64)

        low, high = banks[:4], banks[4:]
        gather_g(0, 0, S)
        load_g(3, "slot_a")
        quantize_wc(1, on_v)
        load_wd(0, "slot_b")
        for b in range(blocks):
            predict(b, "b", banks[b])
        for b in range(blocks):
            predict(b, "a", banks[b])
        for b in range(blocks):
            turn(b, banks[b])
        gather_g(1, 0, S)
        load_wd(1, "slot_c")
        gather_g(2, 0, S)
        load_wd(2, "slot_d")
        gather_g(PACK - 1, 0, HALF // 2)
        gather_g(PACK - 1, HALF // 2, HALF)
        for r in range(per_half):
            add_latents(r)
        wd16 = g_flat[:, PACK * S - HALF :].bitcast(BF16)
        quantize_wd(0, 0, 1, wd16[:, 2 * KP :], on_s)
        quantize_z(0)
        quantize_wd(0, 1, 2, wd16[:, : 2 * KP], on_s)
        y00 = slot("y00", "slot_b", [P, PACK, HALF], F32)
        project_half(0, 0, low, y00[:], 0, 2)
        gather_g(PACK - 1, HALF, S - HALF // 2)
        gather_g(PACK - 1, S - HALF // 2, S)
        wd16 = half16("wd16", "wc16_0")
        round_wd(1, 0, 2, wd16[:], on_s, 0, SHARE)
        round_wd(1, 0, 2, wd16[:], on_v, SHARE, P)
        quantize(wd_q[1][0][:], wd_q[1][1][:], wd16[:])
        for r in range(per_half):
            add_latents(per_half + r)

        def y_tile():
            return ring.tile([P, PACK, HALF], F32, name="y", tag="big", bufs=3)[:]

        units = [project_half(0, 0, low, y00[:], 2, PACK), project_half(0, 1, low, y_tile())]
        quantize_z(1)
        units.append(project_half(1, 0, low, y_tile()))
        y16 = {(0, 0): weave(units[0], half16("y16", "h16")[:], on_v)}
        wd16 = half16("wd16", "h16")
        for u in range(2):
            round_wd(2, u, u + 1, wd16[:, 2 * KP * u : 2 * KP * (u + 1)], on_v)
        planes(0, 0, y16[0, 0])
        nc.vector.quantize_mx(out=wd_q[2][0][:].bitcast(FP8X4), scales=wd_q[2][1][:], in_=wd16[:])
        units.append(project_half(1, 1, low, y_tile()))
        project_pair(2, 0, g_pick)
        project_pair(2, 1, g_pick)
        units.extend(g_pick[:, :, h * HALF : (h + 1) * HALF] for h in range(halves))
        y16[1, 0] = weave(units[2], half16("y16", "h16")[:], on_v)
        y16[0, 1] = weave(units[1], half16("y16", "h16")[:], on_v)
        planes(1, 0, y16[1, 0])
        nc.sync.dma_start(words32[0], y_c[0][:].bitcast(I32))
        y16[1, 1] = weave(units[3], half16("y16", "h16")[:], on_v)
        planes(0, 1, y16[0, 1])
        planes(1, 1, y16[1, 1])
        nc.sync.dma_start(words32[1], y_c[1][:].bitcast(I32))
        store_scales(0, groups - 1, y_early, 4, [nc.sync])
        y16[0, 2] = weave(units[4], half16("y16", "h16")[:], on_v)
        last = half16("y16", "wc16_0")[:]
        weave(units[5][:, :, :LAST], last[:, : PACK * LAST], on_v)
        weave(units[5][:, :, LAST:], last[:, PACK * LAST :], on_s)
        planes(0, 2, y16[0, 2])
        planes(1, 2, last)
        store_scales(groups - 1, groups, y_last, 8, [nc.scalar, nc.sync])
